import numpy as np
import ml_dtypes


def mxq(x, axis, fmt="e4m3"):
    dtype, down = {"e4m3": (ml_dtypes.float8_e4m3fn, 7), "e5m2": (ml_dtypes.float8_e5m2, 14)}[fmt]
    v = np.moveaxis(np.asarray(x, np.float32).astype(ml_dtypes.bfloat16).astype(np.float64), axis, -1)
    blocks = v.reshape(v.shape[:-1] + (-1, 32))
    amax = np.abs(blocks).max(-1, keepdims=True)
    byte = np.maximum(np.where(amax > 0, np.frexp(amax)[1] - 1 + 127, 0) - down, 1)
    scale = np.exp2(byte - 127.0)
    codes = (blocks / scale).astype(np.float32).astype(dtype).astype(np.float64)
    return np.moveaxis((codes * scale).reshape(v.shape), -1, axis)


WIDE = False


def mx_kscale(k):
    if not WIDE:
        return np.ones(k)
    levels = np.array([10, -10, 5, -5, 0])
    if k % 512:
        return np.exp2(np.random.permutation(np.resize(levels, k // 32))).repeat(32)
    a = np.empty((k // 512, 16))
    for p in range(k // 512):
        a[p, :8] = np.random.permutation(np.resize(levels, 8))
        for g in range(8):
            far = levels[np.abs(levels - a[p, g]) >= 10]
            a[p, g + 8] = far[np.random.randint(len(far))]
    return np.exp2(a.ravel()).repeat(32)


BF16 = ml_dtypes.bfloat16


def bf(x):
    return np.asarray(x, np.float32).astype(BF16)


def f64(x):
    return np.asarray(x).astype(np.float64)


E2M1 = np.array([0.0, 0.5, 1.0, 1.5, 2.0, 3.0, 4.0, 6.0, -0.0, -0.5, -1.0, -1.5, -2.0, -3.0, -4.0, -6.0])


def pack_weight(w, fmt):
    k, n = w.shape
    w = f64(bf(w)).reshape(k // 32, 32, n)
    amax = np.abs(w).max(1)
    if fmt == "e4m3":
        byte = np.frexp(amax)[1] - 1 + 127 - 7
    else:
        mant, ex = np.frexp(amax / 6.0)
        byte = np.where(mant > 0.5, ex, ex - 1) + 127
    byte = np.clip(np.where(amax > 0, byte, 1), 1, 254)
    scaled = (w * np.exp2(127.0 - byte)[:, None, :]).reshape(k, n).astype(np.float32)
    by_word = np.ascontiguousarray(scaled.reshape(k // 512, 128, 4, n).transpose(0, 1, 3, 2))
    if fmt == "e4m3":
        words = by_word.astype(ml_dtypes.float8_e4m3fn).view(np.uint8)
    else:
        c = by_word.astype(ml_dtypes.float4_e2m1fn).view(np.uint8) & 0xF
        words = c[..., 0::2] | (c[..., 1::2] << 4)
    return np.ascontiguousarray(words), np.ascontiguousarray(byte.astype(np.uint8).reshape(k // 512, 16, n))


def unpack_weight(words, scales, fmt):
    g, p, n, _ = words.shape
    if fmt == "e4m3":
        vals = np.ascontiguousarray(words).view(ml_dtypes.float8_e4m3fn).astype(np.float64)
    else:
        nib = np.empty((g, p, n, 4), np.uint8)
        nib[..., 0::2] = words & 0xF
        nib[..., 1::2] = words >> 4
        vals = E2M1[nib]
    vals = vals * np.repeat(np.exp2(scales.astype(np.float64) - 127.0), 8, axis=1)[..., None]
    return vals.transpose(0, 1, 3, 2).reshape(g * 512, n)


N, C, H, D = 1024, 1024, 1024, 1024


def draw0():
    s, t = mx_kscale(C), mx_kscale(N)
    bt = bf(np.random.standard_normal((N, C)) * s)
    b0 = bf(np.random.standard_normal((N, C)) * s)
    y_words, y_scales = pack_weight(np.random.standard_normal((C, H)) / np.sqrt(C) / s[:, None], "e4m3")
    return {"bt": bt,
            "b0": b0,
            "y_words": y_words,
            "y_scales": y_scales,
            "e": bf(np.random.uniform(0.1, 0.9, (N, H))),
            "x": bf(np.random.standard_normal((N, D)) / t[:, None]),
            "m": bf((1.0 + 0.1 * np.random.standard_normal(N)) * t)}


def burst_probability(gain, drive):
    return 1.0 / (1.0 + np.exp(-(gain * drive)))


def core(bt, b0, y_words, y_scales, e, x, m):
    n = x.shape[0]
    e, m = f64(e), f64(m)
    yq = unpack_weight(y_words, y_scales, "e4m3")
    ut = mxq(f64(bt), 1, "e4m3") @ yq
    u0 = mxq(f64(b0), 1, "e4m3") @ yq
    k = 4.0 * (1.0 - e)
    dp = burst_probability(k, ut) - burst_probability(k, u0)
    delta = m[:, None] * e * dp
    return (mxq(f64(x), 0, "e4m3").T @ mxq(delta, 0, "e4m3")) / np.sqrt(n)


def e4m3fn_bytes(y):
    return np.clip(np.asarray(y, np.float64), -448.0, 448.0).astype(np.float32).astype(ml_dtypes.float8_e4m3fn).view(np.uint8)


def e4m3fn_values(b):
    return np.asarray(b, np.uint8).view(ml_dtypes.float8_e4m3fn).astype(np.float64)


def setup_inputs():
    d = draw0()
    x0 = np.asarray(d['x']).astype(np.float64)
    s = (np.max(np.abs(x0), axis=(1,), keepdims=True) / 448.0).astype(np.float32)
    out = {}
    for k, v in d.items():
        if k == 'x':
            out['x_bytes'] = e4m3fn_bytes(x0 / s.astype(np.float64))
            out['x_scale'] = s
        else:
            out[k] = v
    return out


def reference(bt, b0, y_words, y_scales, e, x_bytes, x_scale, m):
    return core(bt, b0, y_words, y_scales, e, e4m3fn_values(x_bytes) * x_scale.astype(np.float64), m)

@@ -1,0 +1,374 @@
+from contextlib import ExitStack
+
+import concourse.mybir as mybir
+from concourse.masks import make_identity
+
+N, C, H, D = 1024, 1024, 1024, 1024
+FLOPS = 3 * 2 * 1024 * 1024 * 1024
+
+F32 = mybir.dt.float32
+BF16 = mybir.dt.bfloat16
+I32 = mybir.dt.int32
+U32 = mybir.dt.uint32
+U8 = mybir.dt.uint8
+FP8 = mybir.dt.float8_e4m3fn
+FP8X4 = mybir.dt.float8_e4m3fn_x4
+ALU = mybir.AluOpType
+ACT = mybir.ActivationFunctionType
+
+P = 128
+PACK = 4
+PASSES = 2
+TILES = PASSES * PACK
+BANK = 512
+CHUNK = 256
+BLOCK = 128
+RUN = 4
+
+
+def tile_burstpropfeedbackdifferenceupdate_w8_kernel(tc, bt, b0, y_words, y_scales, e, x_bytes, x_scale, m, out):
+    nc = tc.nc
+    with ExitStack() as ctx:
+        keep = ctx.enter_context(tc.tile_pool(name="keep", bufs=1))
+        stream = ctx.enter_context(tc.tile_pool(name="stream", bufs=2))
+        psum = ctx.enter_context(tc.psum_pool(name="psum", bufs=1))
+        ctx.enter_context(tc.manual_schedule())
+
+        def kept(name, shape, dtype):
+            return keep.tile(shape, dtype, name=name, align_bytes=64)
+
+        identity = kept("identity", [P, P], F32)
+        y_planes = kept("y_planes", [P, PASSES, H], U8)
+        y_codes = [kept("y_codes%d" % i, [P, PASSES, H // 2], U32) for i in range(2)]
+        x_scale_sb = kept("x_scale_sb", [P, TILES], F32)
+        m_sb = kept("m_sb", [P, TILES], BF16)
+        m_diag = kept("m_diag", [P, TILES, P], BF16)
+        e_first = [kept("e_first%d" % t, [P, H], BF16) for t in range(PACK)]
+        e_second = kept("e_second", [P, PACK * H], BF16)
+        e_blocks = e_second[:].rearrange("p (b t h) -> p b t h", t=PACK, h=BLOCK)
+        x_raw = [kept("x_raw%d" % g, [P, 2 * D], U8) for g in range(2 * PASSES)]
+        x_wide = [kept("x_wide%d" % g, [P, PACK * D], BF16) for g in range(PASSES)]
+        x_codes = [kept("x_codes%d" % g, [P, D], U32) for g in range(PASSES)]
+        x_planes = [kept("x_planes%d" % g, [P, D], U8) for g in range(PASSES)]
+        b_codes = [kept("b_codes%d" % j, [P, 2 * PASSES * P], U32) for j in range(TILES)]
+        b_planes = [kept("b_planes%d" % j, [P, 2 * PASSES * P], U8) for j in range(TILES)]
+        delta_codes = kept("delta_codes", [P, TILES * 2 * BLOCK], U32)
+        delta_planes = kept("delta_planes", [P, TILES * 2 * BLOCK], U8)
+        dp_first = kept("dp_first", [P, PACK * H], F32)
+        warm = kept("warm", [P, 2], F32)
+        zeros = kept("zeros", [P, BANK], BF16)
+
+        b_rows = {}
+        banks = {}
+        staged = {}
+
+        def bank_tile(number, shape):
+            return psum.tile(shape, F32, name="bank%d" % number)
+
+        def load_b(j):
+            g, t = divmod(j, PACK)
+            for k, src in enumerate((bt, b0)):
+                rows = stream.tile([P, C], BF16, name="b_rows", bufs=16, align_bytes=64)
+                nc.sync.dma_start(out=rows[:], in_=src.rearrange("(g p t) c -> g t p c", p=P, t=PACK)[g, t])
+                b_rows[j, k] = rows
+
+        def load_y(i):
+            words = y_words.rearrange("g p n t -> p g (n t)")[:, :, i * 2 * H : (i + 1) * 2 * H]
+            nc.sync.dma_start(out=y_codes[i][:].bitcast(I32), in_=words.bitcast(I32))
+
+        def load_e(t):
+            nc.sync.dma_start(out=e_first[t][:], in_=e.rearrange("(g p t) h -> g t p h", p=P, t=PACK)[0, t])
+
+        def load_x(g, a):
+            nc.sync.dma_start(out=x_raw[2 * g + a][:], in_=x_bytes.rearrange("(g p a t) d -> g a p (t d)", p=P, a=2, t=2)[g, a])
+
+        def turn(j):
+            for k in range(2):
+                words = b_rows[j, k][:].bitcast(F32)
+                bank = bank_tile(4 + 2 * (j % 2) + k, [P, PASSES, 2, P])
+                for g in range(PASSES):
+                    for u in range(2):
+                        nc.tensor.transpose(bank[:, g, u, :], words[:, 256 * g + u : 256 * (g + 1) : 2], identity[:])
+                banks["turn", j, k] = bank
+
+        def stage_tile():
+            tile = stream.tile([P, H], F32, name="stage", bufs=3, align_bytes=64)
+            return tile[:]
+
+        def empty_turn(j, where, on_vector=()):
+            staged["b", j] = where
+            for k in range(2):
+                dst = where[:, k * BANK : (k + 1) * BANK].rearrange("p (g r u) -> p g r u", g=PASSES, u=2)
+                src = banks["turn", j, k][:].rearrange("p g u r -> p g r u")
+                if k not in on_vector:
+                    nc.scalar.copy(out=dst, in_=src)
+                else:
+                    nc.vector.tensor_copy(out=dst, in_=src)
+
+        def quantize_b(j, parts=1):
+            src = staged["b", j].bitcast(BF16)
+            w = BANK // parts
+            for k in range(parts):
+                nc.vector.quantize_mx(out=b_codes[j][:, k * w : (k + 1) * w].bitcast(FP8X4), scales=b_planes[j][:, k * w : (k + 1) * w],
+                                      in_=src[:, 4 * k * w : 4 * (k + 1) * w])
+
+        def widen_x(j, on_vector):
+            g, t = divmod(j, PACK)
+            src = x_raw[j // 2][:, (j % 2) * D : (j % 2 + 1) * D].bitcast(FP8)
+            dst = x_wide[g][:, t * D : (t + 1) * D]
+            if on_vector:
+                nc.vector.tensor_scalar(out=dst, in0=src, scalar1=x_scale_sb[:, j : j + 1], scalar2=None, op0=ALU.mult)
+            else:
+                nc.scalar.activation(out=dst, in_=src, func=ACT.Copy, scale=x_scale_sb[:, j : j + 1])
+
+        def weave_x(g, half, where, on_vector=True):
+            staged["x", g, half] = where
+            src = x_wide[g][:].rearrange("p (t a c i) -> p a c t i", t=PACK, a=2, i=RUN)[:, half]
+            dst = where.bitcast(BF16).rearrange("p (c i t) -> p c t i", t=PACK, i=RUN)
+            if on_vector:
+                nc.vector.tensor_copy(out=dst, in_=src)
+            else:
+                nc.scalar.copy(out=dst, in_=src)
+
+        def quantize_x(g, half):
+            cols = slice(half * BANK, (half + 1) * BANK)
+            nc.vector.quantize_mx(out=x_codes[g][:, cols].bitcast(FP8X4), scales=x_planes[g][:, cols], in_=staged["x", g, half].bitcast(BF16))
+
+        def drive_group(dst, j, k, h0, width):
+            i, c0 = divmod(h0, H // 2)
+            for g in range(PASSES):
+                cols = slice((k * PASSES + g) * P, (k * PASSES + g + 1) * P)
+                nc.tensor.matmul_mx(out=dst, lhsT=b_codes[j][:, cols].bitcast(FP8X4), lhsT_scale=b_planes[j][:, cols],
+                                    rhs=y_codes[i][:, g, c0 : c0 + width].bitcast(FP8X4), rhs_scale=y_planes[:, g, h0 : h0 + width],
+                                    start=(g == 0), stop=(g == PASSES - 1))
+
+        def drives_first(t, c):
+            bank = bank_tile(c, [P, 2, CHUNK])
+            for k in range(2):
+                drive_group(bank[:, k, :], t, k, c * CHUNK, CHUNK)
+            banks["drive", 0, t, c] = bank
+
+        def drives_second(b, a):
+            bank = bank_tile((2 * b + a) % 4, [P, 2, 2, BLOCK])
+            for u in range(2):
+                for k in range(2):
+                    drive_group(bank[:, k, u, :], PACK + 2 * a + u, k, b * BLOCK, BLOCK)
+            banks["drive", 1, b, a] = bank
+
+        def gate(dst, e_part, bank):
+            nc.vector.scalar_tensor_tensor(out=dst, in0=e_part.unsqueeze(1).broadcast_to([P, 2, CHUNK]), scalar=1.0, in1=bank, op0=ALU.subtract, op1=ALU.mult)
+
+        def sigmoid(prob, pre, lo, hi):
+            nc.scalar.activation(out=prob[:, :, lo:hi], in_=pre[:, :, lo:hi], func=ACT.Sigmoid, scale=-4.0)
+
+        def difference(dst, prob, engine, lo, hi):
+            engine.tensor_tensor(out=dst[:, lo:hi], in0=prob[:, 0, lo:hi], in1=prob[:, 1, lo:hi], op=ALU.subtract)
+
+        def warm_up(count):
+            bank = bank_tile(3, [P, BANK])
+            for n in range(count):
+                nc.tensor.matmul(bank[:], lhsT=zeros[:, :P], rhs=zeros[:], start=True, stop=True)
+
+        def modulation(g, b, number):
+            bank = bank_tile(number, [P, PACK, BLOCK])
+            for t in range(PACK):
+                rows = e_first[t][:, b * BLOCK : (b + 1) * BLOCK] if g == 0 else e_blocks[:, b, t, :]
+                nc.tensor.matmul(bank[:, t, :], lhsT=m_diag[:, g * PACK + t, :], rhs=rows, start=True, stop=True)
+            banks["mod", g, b] = bank
+
+        def delta(g, b, dp, dst):
+            nc.vector.tensor_tensor(out=dst.rearrange("p (c i t) -> p c t i", t=PACK, i=RUN), in0=dp.rearrange("p t (c i) -> p c t i", i=RUN),
+                                    in1=banks["mod", g, b][:].rearrange("p t (c i) -> p c t i", i=RUN), op=ALU.mult)
+
+        def update(b, a, number):
+            bank = bank_tile(number, [P, PACK, BLOCK])
+            for u in range(PACK):
+                cols = slice((a * PACK + u) * P, (a * PACK + u + 1) * P)
+                for g in range(PASSES):
+                    moving = slice((2 * b + g) * BLOCK, (2 * b + g + 1) * BLOCK)
+                    nc.tensor.matmul_mx(out=bank[:, u, :], lhsT=x_codes[g][:, cols].bitcast(FP8X4), lhsT_scale=x_planes[g][:, cols],
+                                        rhs=delta_codes[:, moving].bitcast(FP8X4), rhs_scale=delta_planes[:, moving],
+                                        start=(g == 0), stop=(g == PASSES - 1))
+            banks["update", b, a] = bank
+
+        def finish(b, a, on_vector):
+            bank = banks["update", b, a]
+            result = stream.tile([P, PACK, BLOCK], F32, name="result", bufs=4)
+            if on_vector:
+                nc.vector.tensor_scalar(out=result[:], in0=bank[:], scalar1=1.0 / 32.0, scalar2=None, op0=ALU.mult)
+            else:
+                nc.scalar.activation(out=result[:], in_=bank[:], func=ACT.Copy, scale=1.0 / 32.0)
+            nc.sync.dma_start(out=out.rearrange("(i p) h -> p i h", p=P)[:, a * PACK : (a + 1) * PACK, b * BLOCK : (b + 1) * BLOCK], in_=result[:])
+
+        nc.gpsimd.dma_start(out=m_sb[:].rearrange("p (g t) -> p g t", t=PACK), in_=m.rearrange("(g p t) -> p g t", p=P, t=PACK))
+        nc.gpsimd.dma_start(out=x_scale_sb[:].rearrange("p (g t) -> p g t", t=PACK), in_=x_scale.rearrange("(g p t) o -> p g (t o)", p=P, t=PACK))
+        make_identity(nc, identity[:])
+        nc.vector.memset(y_planes[:].rearrange("p g n -> p (g n)").bitcast(I32), 0)
+        nc.vector.memset(zeros[:], 0.0)
+        load_b(0)
+        load_x(0, 0)
+        load_y(0)
+        for q in range(4):
+            nc.scalar.dma_start(out=y_planes[32 * q : 32 * q + 4].bitcast(I32), in_=y_scales[:, 4 * q : 4 * q + 4, :].rearrange("g r n -> r g n").bitcast(I32))
+        nc.scalar.activation(out=warm[:], in_=zeros[:, :2], func=ACT.Sigmoid)
+        load_e(0)
+        load_b(1)
+        load_x(0, 1)
+        load_y(1)
+        load_b(2)
+        load_e(1)
+        load_b(3)
+        load_b(4)
+        load_x(1, 0)
+        load_b(5)
+        load_e(2)
+        load_x(1, 1)
+        load_b(6)
+        load_b(7)
+        load_e(3)
+        for t in range(PACK):
+            nc.sync.dma_start(out=e_blocks[:, :, t, :], in_=e.rearrange("(g p t) (b h) -> g t p b h", p=P, t=PACK, h=BLOCK)[1, t])
+
+        dp_region = [dp_first[:, t * H : (t + 1) * H] for t in range(PACK)]
+        nc.vector.tensor_tensor(out=m_diag[:], in0=identity[:].unsqueeze(1).broadcast_to([P, TILES, P]), in1=m_sb[:].unsqueeze(2).broadcast_to([P, TILES, P]), op=ALU.mult)
+        warm_up(4)
+        turn(0)
+        warm_up(3)
+        empty_turn(0, stage_tile())
+        widen_x(0, True)
+        quantize_b(0, 2)
+        widen_x(1, False)
+        drives_first(0, 0)
+        drives_first(0, 1)
+        turn(1)
+        empty_turn(1, stage_tile())
+        drives_first(0, 2)
+        drives_first(0, 3)
+
+        turns = [[2, 3], [4, 5], [6, 7], []]
+        for t in range(PACK):
+            pre = stream.tile([P, 2, H], F32, name="pre")
+            prob = stream.tile([P, 2, H], F32, name="prob")
+            if turns[t] and t:
+                turn(turns[t][0])
+            for c in range(4):
+                gate(pre[:, :, c * CHUNK : (c + 1) * CHUNK], e_first[t][:, c * CHUNK : (c + 1) * CHUNK], banks["drive", 0, t, c][:])
+                if t == 0 and c == 1:
+                    widen_x(2, True)
+                    quantize_b(1)
+                    drives_first(1, 0)
+                    drives_first(1, 1)
+                    turn(2)
+                if c % 2 == 1:
+                    sigmoid(prob, pre, (c - 1) * CHUNK, (c + 1) * CHUNK)
+                if t == 0 and c == 1:
+                    widen_x(3, False)
+                    empty_turn(2, stage_tile())
+                if t == 0:
+                    if c >= 2:
+                        drives_first(1, c)
+                    continue
+                if c == 2 and turns[t]:
+                    turn(turns[t][-1])
+                if t < 3:
+                    drives_first(t + 1, c)
+                elif c == 1:
+                    drives_second(0, 0)
+            if t == 0:
+                turn(3)
+                weave_x(0, 0, dp_region[0])
+                quantize_b(2)
+                quantize_x(0, 0)
+                empty_turn(3, stage_tile())
+                widen_x(4, False)
+            elif t == 1:
+                weave_x(0, 1, dp_region[1])
+                quantize_b(3)
+                quantize_x(0, 1)
+                empty_turn(4, stage_tile())
+                empty_turn(5, dp_region[2])
+            elif t == 2:
+                widen_x(5, True)
+                quantize_b(4)
+                quantize_b(5)
+                empty_turn(6, stage_tile())
+                empty_turn(7, dp_region[3])
+            else:
+                quantize_b(6)
+                widen_x(6, True)
+                quantize_b(7)
+                drives_second(1, 0)
+                drives_second(0, 1)
+                drives_second(1, 1)
+                widen_x(7, False)
+            difference(dp_region[t], prob, nc.gpsimd, 0, H)
+
+        dp_view = dp_first[:].rearrange("p (t h) -> p t h", t=PACK)
+        dp_second = {}
+        woven = {}
+        ups = [(b, a) for b in range(TILES) for a in range(2)]
+        share = {2: 1, 3: 2, 4: 1, 5: 2, 6: 3, 7: 3}
+        started = []
+
+        def quantize_delta(b):
+            cols = slice(2 * b * BLOCK, 2 * (b + 1) * BLOCK)
+            nc.vector.quantize_mx(out=delta_codes[:, cols].bitcast(FP8X4), scales=delta_planes[:, cols], in_=woven[b][:])
+
+        def deltas(b, which):
+            if which == 0:
+                woven[b] = stream.tile([P, 2 * BANK], BF16, name="woven", align_bytes=64)
+                delta(0, b, dp_view[:, :, b * BLOCK : (b + 1) * BLOCK], woven[b][:, :BANK])
+            else:
+                delta(1, b, dp_second[b][:].rearrange("p (t h) -> p t h", t=PACK), woven[b][:, BANK:])
+
+        for s in range(TILES):
+            pre = stream.tile([P, 2, BANK], F32, name="pre")
+            prob = stream.tile([P, 2, BANK], F32, name="prob")
+            if s >= 1:
+                modulation(0, s - 1, 4)
+                modulation(1, s - 1, 5)
+            for a in range(2):
+                gate(pre[:, :, a * CHUNK : (a + 1) * CHUNK], e_blocks[:, s, 2 * a : 2 * a + 2, :].rearrange("p t h -> p (t h)"),
+                     banks["drive", 1, s, a][:].rearrange("p k u h -> p k (u h)"))
+                sigmoid(prob, pre, a * CHUNK, (a + 1) * CHUNK)
+                if s + 2 < TILES and a == 0:
+                    drives_second(s + 2, 0)
+            if s == TILES - 1:
+                modulation(0, s, 0)
+                modulation(1, s, 1)
+            dp_second[s] = stream.tile([P, BANK], F32, name="dp_second")
+            difference(dp_second[s], prob, nc.gpsimd, 0, BANK)
+            if s == 0:
+                weave_x(1, 1, stage_tile(), False)
+            if s == 1:
+                weave_x(1, 0, stage_tile(), True)
+            if s == 2:
+                quantize_x(1, 1)
+            if s >= 3:
+                finish(s - 3, 1, False)
+            if s >= 2:
+                quantize_delta(s - 2)
+                update(s - 2, 0, 6)
+                finish(s - 2, 0, False)
+            if s + 2 < TILES:
+                drives_second(s + 2, 1)
+            if s >= 1:
+                deltas(s - 1, 0)
+                if s == 1:
+                    quantize_x(1, 0)
+                deltas(s - 1, 1)
+            if s >= 2:
+                update(s - 2, 1, 7)
+        deltas(TILES - 1, 0)
+        quantize_delta(TILES - 2)
+        update(TILES - 2, 0, 2)
+        update(TILES - 2, 1, 3)
+        finish(TILES - 3, 1, False)
+        deltas(TILES - 1, 1)
+        finish(TILES - 2, 0, False)
+        quantize_delta(TILES - 1)
+        update(TILES - 1, 0, 4)
+        update(TILES - 1, 1, 5)
+        finish(TILES - 2, 1, True)
+        finish(TILES - 1, 0, False)
+        finish(TILES - 1, 1, True)

@@ -45,15 +45,15 @@ def tile_burstpropfeedbackdifferenceupdate_w8_kernel(tc, bt, b0, y_words, y_scal
         m_diag = kept("m_diag", [P, TILES, P], BF16)
         e_first = [kept("e_first%d" % t, [P, H], BF16) for t in range(PACK)]
         e_second = kept("e_second", [P, PACK * H], BF16)
-        e_blocks = e_second[:].rearrange("p (b t h) -> p b t h", t=PACK, h=BLOCK)
+        e_rows = [e_first[t][:] for t in range(PACK)] + [e_second[:, t * H : (t + 1) * H] for t in range(PACK)]
         x_raw = [kept("x_raw%d" % g, [P, 2 * D], U8) for g in range(2 * PASSES)]
         x_wide = [kept("x_wide%d" % g, [P, PACK * D], BF16) for g in range(PASSES)]
         x_codes = [kept("x_codes%d" % g, [P, D], U32) for g in range(PASSES)]
         x_planes = [kept("x_planes%d" % g, [P, D], U8) for g in range(PASSES)]
         b_codes = [kept("b_codes%d" % j, [P, 2 * PASSES * P], U32) for j in range(TILES)]
         b_planes = [kept("b_planes%d" % j, [P, 2 * PASSES * P], U8) for j in range(TILES)]
-        delta_codes = kept("delta_codes", [P, TILES * 2 * BLOCK], U32)
-        delta_planes = kept("delta_planes", [P, TILES * 2 * BLOCK], U8)
+        delta_codes = [kept("delta_codes%d" % g, [P, H], U32) for g in range(PASSES)]
+        delta_planes = [kept("delta_planes%d" % g, [P, H], U8) for g in range(PASSES)]
         dp_first = kept("dp_first", [P, PACK * H], F32)
         warm = kept("warm", [P, 2], F32)
         zeros = kept("zeros", [P, BANK], BF16)
@@ -121,11 +121,16 @@ def tile_burstpropfeedbackdifferenceupdate_w8_kernel(tc, bt, b0, y_words, y_scal
             else:
                 nc.scalar.activation(out=dst, in_=src, func=ACT.Copy, scale=x_scale_sb[:, j : j + 1])
 
-        def weave_x(g, half, where, on_vector=True):
+        def weave_x(g, half, where, engine, lo=0, hi=BANK):
             staged["x", g, half] = where
-            src = x_wide[g][:].rearrange("p (t a c i) -> p a c t i", t=PACK, a=2, i=RUN)[:, half]
-            dst = where.bitcast(BF16).rearrange("p (c i t) -> p c t i", t=PACK, i=RUN)
-            if on_vector:
+            src = x_wide[g][:].rearrange("p (t a d) -> p a t d", t=PACK, a=2)[:, half, :, lo:hi]
+            dst = where.bitcast(BF16)[:, PACK * lo : PACK * hi]
+            if engine == "gpsimd":
+                nc.gpsimd.tensor_scalar(out=dst.rearrange("p (d t) -> p d t", t=PACK), in0=src.rearrange("p t d -> p d t"), scalar1=1.0, scalar2=0.0, op0=ALU.mult, op1=ALU.add)
+                return
+            src = src.rearrange("p t (c i) -> p c t i", i=RUN)
+            dst = dst.rearrange("p (c i t) -> p c t i", t=PACK, i=RUN)
+            if engine == "vector":
                 nc.vector.tensor_copy(out=dst, in_=src)
             else:
                 nc.scalar.copy(out=dst, in_=src)
@@ -142,21 +147,15 @@ def tile_burstpropfeedbackdifferenceupdate_w8_kernel(tc, bt, b0, y_words, y_scal
                                     rhs=y_codes[i][:, g, c0 : c0 + width].bitcast(FP8X4), rhs_scale=y_planes[:, g, h0 : h0 + width],
                                     start=(g == 0), stop=(g == PASSES - 1))
 
-        def drives_first(t, c):
-            bank = bank_tile(c, [P, 2, CHUNK])
+        def drives(j, c, number):
+            bank = bank_tile(number, [P, 2, CHUNK])
             for k in range(2):
-                drive_group(bank[:, k, :], t, k, c * CHUNK, CHUNK)
-            banks["drive", 0, t, c] = bank
+                drive_group(bank[:, k, :], j, k, c * CHUNK, CHUNK)
+            banks["drive", j, c] = bank
 
-        def drives_second(b, a):
-            bank = bank_tile((2 * b + a) % 4, [P, 2, 2, BLOCK])
-            for u in range(2):
-                for k in range(2):
-                    drive_group(bank[:, k, u, :], PACK + 2 * a + u, k, b * BLOCK, BLOCK)
-            banks["drive", 1, b, a] = bank
-
-        def gate(dst, e_part, bank):
-            nc.vector.scalar_tensor_tensor(out=dst, in0=e_part.unsqueeze(1).broadcast_to([P, 2, CHUNK]), scalar=1.0, in1=bank, op0=ALU.subtract, op1=ALU.mult)
+        def gate(pre, slot, j, c):
+            nc.vector.scalar_tensor_tensor(out=pre[:, :, slot * CHUNK : (slot + 1) * CHUNK], in0=e_rows[j][:, c * CHUNK : (c + 1) * CHUNK].unsqueeze(1).broadcast_to([P, 2, CHUNK]),
+                                           scalar=1.0, in1=banks["drive", j, c][:], op0=ALU.subtract, op1=ALU.mult)
 
         def sigmoid(prob, pre, lo, hi):
             nc.scalar.activation(out=prob[:, :, lo:hi], in_=pre[:, :, lo:hi], func=ACT.Sigmoid, scale=-4.0)
@@ -172,7 +171,7 @@ def tile_burstpropfeedbackdifferenceupdate_w8_kernel(tc, bt, b0, y_words, y_scal
         def modulation(g, b, number):
             bank = bank_tile(number, [P, PACK, BLOCK])
             for t in range(PACK):
-                rows = e_first[t][:, b * BLOCK : (b + 1) * BLOCK] if g == 0 else e_blocks[:, b, t, :]
+                rows = e_rows[g * PACK + t][:, b * BLOCK : (b + 1) * BLOCK]
                 nc.tensor.matmul(bank[:, t, :], lhsT=m_diag[:, g * PACK + t, :], rhs=rows, start=True, stop=True)
             banks["mod", g, b] = bank
 
@@ -180,25 +179,27 @@ def tile_burstpropfeedbackdifferenceupdate_w8_kernel(tc, bt, b0, y_words, y_scal
             nc.vector.tensor_tensor(out=dst.rearrange("p (c i t) -> p c t i", t=PACK, i=RUN), in0=dp.rearrange("p t (c i) -> p c t i", i=RUN),
                                     in1=banks["mod", g, b][:].rearrange("p t (c i) -> p c t i", i=RUN), op=ALU.mult)
 
-        def update(b, a, number):
-            bank = bank_tile(number, [P, PACK, BLOCK])
-            for u in range(PACK):
-                cols = slice((a * PACK + u) * P, (a * PACK + u + 1) * P)
+        def update(h0, width, i0, count, number):
+            bank = bank_tile(number, [P, count, width])
+            for u in range(count):
+                cols = slice((i0 + u) * P, (i0 + u + 1) * P)
                 for g in range(PASSES):
-                    moving = slice((2 * b + g) * BLOCK, (2 * b + g + 1) * BLOCK)
                     nc.tensor.matmul_mx(out=bank[:, u, :], lhsT=x_codes[g][:, cols].bitcast(FP8X4), lhsT_scale=x_planes[g][:, cols],
-                                        rhs=delta_codes[:, moving].bitcast(FP8X4), rhs_scale=delta_planes[:, moving],
+                                        rhs=delta_codes[g][:, h0 : h0 + width].bitcast(FP8X4), rhs_scale=delta_planes[g][:, h0 : h0 + width],
                                         start=(g == 0), stop=(g == PASSES - 1))
-            banks["update", b, a] = bank
+            banks["update", h0, i0] = bank
 
-        def finish(b, a, on_vector):
-            bank = banks["update", b, a]
-            result = stream.tile([P, PACK, BLOCK], F32, name="result", bufs=4)
+        def finish(h0, width, i0, count, on_vector):
+            bank = banks["update", h0, i0]
+            result = stream.tile([P, count, width], F32, name="result", bufs=6)
             if on_vector:
                 nc.vector.tensor_scalar(out=result[:], in0=bank[:], scalar1=1.0 / 32.0, scalar2=None, op0=ALU.mult)
             else:
                 nc.scalar.activation(out=result[:], in_=bank[:], func=ACT.Copy, scale=1.0 / 32.0)
-            nc.sync.dma_start(out=out.rearrange("(i p) h -> p i h", p=P)[:, a * PACK : (a + 1) * PACK, b * BLOCK : (b + 1) * BLOCK], in_=result[:])
+            nc.sync.dma_start(out=out.rearrange("(i p) h -> p i h", p=P)[:, i0 : i0 + count, h0 : h0 + width], in_=result[:])
+
+        def quantize_delta(g, h0, width, src):
+            nc.vector.quantize_mx(out=delta_codes[g][:, h0 : h0 + width].bitcast(FP8X4), scales=delta_planes[g][:, h0 : h0 + width], in_=src)
 
         nc.gpsimd.dma_start(out=m_sb[:].rearrange("p (g t) -> p g t", t=PACK), in_=m.rearrange("(g p t) -> p g t", p=P, t=PACK))
         nc.gpsimd.dma_start(out=x_scale_sb[:].rearrange("p (g t) -> p g t", t=PACK), in_=x_scale.rearrange("(g p t) o -> p g (t o)", p=P, t=PACK))
@@ -213,21 +214,20 @@ def tile_burstpropfeedbackdifferenceupdate_w8_kernel(tc, bt, b0, y_words, y_scal
         nc.scalar.activation(out=warm[:], in_=zeros[:, :2], func=ACT.Sigmoid)
         load_e(0)
         load_b(1)
-        load_x(0, 1)
         load_y(1)
+        load_x(0, 1)
         load_b(2)
         load_e(1)
         load_b(3)
-        load_b(4)
         load_x(1, 0)
-        load_b(5)
+        load_b(4)
         load_e(2)
+        load_b(5)
         load_x(1, 1)
         load_b(6)
-        load_b(7)
         load_e(3)
-        for t in range(PACK):
-            nc.sync.dma_start(out=e_blocks[:, :, t, :], in_=e.rearrange("(g p t) (b h) -> g t p b h", p=P, t=PACK, h=BLOCK)[1, t])
+        load_b(7)
+        nc.sync.dma_start(out=e_second[:], in_=e.rearrange("(g p t) h -> g p (t h)", p=P, t=PACK)[1])
 
         dp_region = [dp_first[:, t * H : (t + 1) * H] for t in range(PACK)]
         nc.vector.tensor_tensor(out=m_diag[:], in0=identity[:].unsqueeze(1).broadcast_to([P, TILES, P]), in1=m_sb[:].unsqueeze(2).broadcast_to([P, TILES, P]), op=ALU.mult)
@@ -238,137 +238,185 @@ def tile_burstpropfeedbackdifferenceupdate_w8_kernel(tc, bt, b0, y_words, y_scal
         widen_x(0, True)
         quantize_b(0, 2)
         widen_x(1, False)
-        drives_first(0, 0)
-        drives_first(0, 1)
+        drives(0, 0, 0)
+        drives(0, 1, 1)
         turn(1)
         empty_turn(1, stage_tile())
-        drives_first(0, 2)
-        drives_first(0, 3)
+        drives(0, 2, 2)
+        drives(0, 3, 3)
 
-        turns = [[2, 3], [4, 5], [6, 7], []]
         for t in range(PACK):
             pre = stream.tile([P, 2, H], F32, name="pre")
             prob = stream.tile([P, 2, H], F32, name="prob")
-            if turns[t] and t:
-                turn(turns[t][0])
+            if t:
+                turn(2 * t + 1)
+                empty_turn(2 * t + 1, dp_region[t] if t > 1 else stage_tile())
             for c in range(4):
-                gate(pre[:, :, c * CHUNK : (c + 1) * CHUNK], e_first[t][:, c * CHUNK : (c + 1) * CHUNK], banks["drive", 0, t, c][:])
+                gate(pre, c, t, c)
                 if t == 0 and c == 1:
                     widen_x(2, True)
-                    quantize_b(1)
-                    drives_first(1, 0)
-                    drives_first(1, 1)
+                    widen_x(3, False)
                     turn(2)
                 if c % 2 == 1:
                     sigmoid(prob, pre, (c - 1) * CHUNK, (c + 1) * CHUNK)
                 if t == 0 and c == 1:
-                    widen_x(3, False)
-                    empty_turn(2, stage_tile())
+                    empty_turn(2, dp_region[0])
                 if t == 0:
-                    if c >= 2:
-                        drives_first(1, c)
                     continue
-                if c == 2 and turns[t]:
-                    turn(turns[t][-1])
                 if t < 3:
-                    drives_first(t + 1, c)
-                elif c == 1:
-                    drives_second(0, 0)
+                    if c == 1:
+                        drives(t + 1, 0, 0)
+                        drives(t + 1, 1, 1)
+                        turn(2 * t + 2)
+                    if c >= 2:
+                        drives(t + 1, c, c)
+                elif c < 2:
+                    drives(PACK + c, 0, c)
+            if 0 < t < 3:
+                empty_turn(2 * t + 2, stage_tile())
             if t == 0:
-                turn(3)
-                weave_x(0, 0, dp_region[0])
+                quantize_b(1)
+                for c in range(4):
+                    drives(1, c, c)
+                weave_x(0, 0, stage_tile(), "vector")
                 quantize_b(2)
-                quantize_x(0, 0)
-                empty_turn(3, stage_tile())
                 widen_x(4, False)
             elif t == 1:
-                weave_x(0, 1, dp_region[1])
+                weave_x(0, 1, dp_region[1], "vector")
+                quantize_x(0, 0)
                 quantize_b(3)
                 quantize_x(0, 1)
-                empty_turn(4, stage_tile())
-                empty_turn(5, dp_region[2])
             elif t == 2:
                 widen_x(5, True)
                 quantize_b(4)
+                widen_x(6, True)
                 quantize_b(5)
-                empty_turn(6, stage_tile())
-                empty_turn(7, dp_region[3])
             else:
                 quantize_b(6)
-                widen_x(6, True)
+                drives(6, 0, 2)
+                widen_x(7, True)
                 quantize_b(7)
-                drives_second(1, 0)
-                drives_second(0, 1)
-                drives_second(1, 1)
-                widen_x(7, False)
-            difference(dp_region[t], prob, nc.gpsimd, 0, H)
+                drives(7, 0, 3)
+            if t < 3:
+                difference(dp_region[t], prob, nc.gpsimd, 0, H)
+            else:
+                difference(dp_region[t], prob, nc.gpsimd, 0, CHUNK)
+                difference(dp_region[t], prob, nc.gpsimd, CHUNK, H)
 
         dp_view = dp_first[:].rearrange("p (t h) -> p t h", t=PACK)
-        dp_second = {}
-        woven = {}
-        ups = [(b, a) for b in range(TILES) for a in range(2)]
-        share = {2: 1, 3: 2, 4: 1, 5: 2, 6: 3, 7: 3}
-        started = []
+        work = [kept("work%d" % c, [P, H], F32) for c in range(5)]
 
-        def quantize_delta(b):
-            cols = slice(2 * b * BLOCK, 2 * (b + 1) * BLOCK)
-            nc.vector.quantize_mx(out=delta_codes[:, cols].bitcast(FP8X4), scales=delta_planes[:, cols], in_=woven[b][:])
+        def delta_first(b):
+            delta(0, b, dp_view[:, :, b * BLOCK : (b + 1) * BLOCK], work[b // 2][:].bitcast(BF16)[:, (b % 2) * BANK : (b % 2 + 1) * BANK])
 
-        def deltas(b, which):
-            if which == 0:
-                woven[b] = stream.tile([P, 2 * BANK], BF16, name="woven", align_bytes=64)
-                delta(0, b, dp_view[:, :, b * BLOCK : (b + 1) * BLOCK], woven[b][:, :BANK])
+        def delta_second(b):
+            dp = work[b // 2][:].rearrange("p (t h) -> p t h", t=PACK)[:, :, (b % 2) * BLOCK : (b % 2 + 1) * BLOCK]
+            delta(1, b, dp, work[b // 2 + 1][:].bitcast(BF16)[:, (2 + b % 2) * BANK : (3 + b % 2) * BANK])
+
+        modulation(0, 0, 4)
+        modulation(0, 1, 5)
+        for c in range(3):
+            pre = stream.tile([P, 2, H], F32, name="pre")
+            prob = stream.tile([P, 2, H], F32, name="prob")
+            done = (c - 2) * CHUNK
+            if c < 2:
+                weave_x(1, c, stage_tile(), "scalar")
             else:
-                delta(1, b, dp_second[b][:].rearrange("p (t h) -> p t h", t=PACK), woven[b][:, BANK:])
-
-        for s in range(TILES):
-            pre = stream.tile([P, 2, BANK], F32, name="pre")
-            prob = stream.tile([P, 2, BANK], F32, name="prob")
-            if s >= 1:
-                modulation(0, s - 1, 4)
-                modulation(1, s - 1, 5)
+                update(done, CHUNK, 0, 2, 6)
+                update(done, CHUNK, 2, 2, 7)
+                finish(done, CHUNK, 0, 2, False)
+                finish(done, CHUNK, 2, 2, False)
+            gate(pre, 0, 4, c)
+            drives(4, c + 1, 0)
+            if c:
+                delta_first(2 * c)
+                modulation(1, 2 * c - 2, 4)
+            gate(pre, 1, 5, c)
+            sigmoid(prob, pre, 0, 2 * CHUNK)
+            drives(5, c + 1, 1)
+            if c:
+                delta_first(2 * c + 1)
+                modulation(1, 2 * c - 1, 5)
+            if c >= 2:
+                update(done, CHUNK, 4, 2, 6)
+                update(done, CHUNK, 6, 2, 7)
+            gate(pre, 2, 6, c)
+            drives(6, c + 1, 2)
+            gate(pre, 3, 7, c)
+            sigmoid(prob, pre, 2 * CHUNK, H)
+            if c >= 2:
+                finish(done, CHUNK, 4, 2, False)
+                finish(done, CHUNK, 6, 2, False)
             for a in range(2):
-                gate(pre[:, :, a * CHUNK : (a + 1) * CHUNK], e_blocks[:, s, 2 * a : 2 * a + 2, :].rearrange("p t h -> p (t h)"),
-                     banks["drive", 1, s, a][:].rearrange("p k u h -> p k (u h)"))
-                sigmoid(prob, pre, a * CHUNK, (a + 1) * CHUNK)
-                if s + 2 < TILES and a == 0:
-                    drives_second(s + 2, 0)
-            if s == TILES - 1:
-                modulation(0, s, 0)
-                modulation(1, s, 1)
-            dp_second[s] = stream.tile([P, BANK], F32, name="dp_second")
-            difference(dp_second[s], prob, nc.gpsimd, 0, BANK)
-            if s == 0:
-                weave_x(1, 1, stage_tile(), False)
-            if s == 1:
-                weave_x(1, 0, stage_tile(), True)
-            if s == 2:
-                quantize_x(1, 1)
-            if s >= 3:
-                finish(s - 3, 1, False)
-            if s >= 2:
-                quantize_delta(s - 2)
-                update(s - 2, 0, 6)
-                finish(s - 2, 0, False)
-            if s + 2 < TILES:
-                drives_second(s + 2, 1)
-            if s >= 1:
-                deltas(s - 1, 0)
-                if s == 1:
-                    quantize_x(1, 0)
-                deltas(s - 1, 1)
-            if s >= 2:
-                update(s - 2, 1, 7)
-        deltas(TILES - 1, 0)
-        quantize_delta(TILES - 2)
-        update(TILES - 2, 0, 2)
-        update(TILES - 2, 1, 3)
-        finish(TILES - 3, 1, False)
-        deltas(TILES - 1, 1)
-        finish(TILES - 2, 0, False)
-        quantize_delta(TILES - 1)
-        update(TILES - 1, 0, 4)
-        update(TILES - 1, 1, 5)
-        finish(TILES - 2, 1, True)
-        finish(TILES - 1, 0, False)
-        finish(TILES - 1, 1, True)
+                if c:
+                    delta_second(2 * c - 2 + a)
+                else:
+                    delta_first(a)
+                modulation(0, 2 * c + 2 + a, 4 + a)
+                if a == 0:
+                    drives(7, c + 1, 3)
+            if c < 2:
+                quantize_x(1, c)
+            quantize_delta(0, c * CHUNK, CHUNK, work[c][:].bitcast(BF16)[:, : 2 * BANK])
+            if c:
+                quantize_delta(1, (c - 1) * CHUNK, CHUNK, work[c][:].bitcast(BF16)[:, 2 * BANK :])
+            difference(work[c], prob, nc.gpsimd, 0, H)
+
+        pre = stream.tile([P, 2, H], F32, name="pre")
+        prob = stream.tile([P, 2, H], F32, name="prob")
+        done = CHUNK
+        update(done, CHUNK, 0, 2, 6)
+        update(done, CHUNK, 2, 2, 7)
+        finish(done, CHUNK, 0, 2, False)
+        finish(done, CHUNK, 2, 2, False)
+        gate(pre, 0, 4, 3)
+        update(done, CHUNK, 4, 2, 0)
+        delta_first(6)
+        modulation(1, 4, 4)
+        gate(pre, 1, 5, 3)
+        sigmoid(prob, pre, 0, 2 * CHUNK)
+        update(done, CHUNK, 6, 2, 1)
+        delta_first(7)
+        modulation(1, 5, 5)
+        finish(done, CHUNK, 4, 2, False)
+        gate(pre, 2, 6, 3)
+        modulation(1, 6, 2)
+        gate(pre, 3, 7, 3)
+        modulation(1, 7, 3)
+        sigmoid(prob, pre, 2 * CHUNK, H)
+        finish(done, CHUNK, 6, 2, False)
+        delta_second(4)
+        delta_second(5)
+        quantize_delta(0, 3 * CHUNK, CHUNK, work[3][:].bitcast(BF16)[:, : 2 * BANK])
+        quantize_delta(1, 2 * CHUNK, CHUNK, work[3][:].bitcast(BF16)[:, 2 * BANK :])
+        done = 2 * CHUNK
+        dp_last = kept("dp_last", [P, PACK, CHUNK], F32)
+        prob_view = prob[:].rearrange("p k (t h) -> p k t h", t=PACK)
+
+        def last_difference(engine, a):
+            cols = slice(a * BLOCK, (a + 1) * BLOCK)
+            engine.tensor_tensor(out=dp_last[:, :, cols], in0=prob_view[:, 0, :, cols], in1=prob_view[:, 1, :, cols], op=ALU.subtract)
+
+        def last_delta(a):
+            delta(1, 6 + a, dp_last[:, :, a * BLOCK : (a + 1) * BLOCK], work[4][:].bitcast(BF16)[:, a * BANK : (a + 1) * BANK])
+
+        update(done, CHUNK, 0, 2, 6)
+        update(done, CHUNK, 2, 2, 7)
+        update(done, CHUNK, 4, 2, 0)
+        update(done, CHUNK, 6, 2, 1)
+        last_difference(nc.vector, 0)
+        last_difference(nc.vector, 1)
+        last_delta(0)
+        for i0 in range(0, TILES, 2):
+            finish(done, CHUNK, i0, 2, False)
+        quantize_delta(1, 6 * BLOCK, BLOCK, work[4][:].bitcast(BF16)[:, :BANK])
+        update(6 * BLOCK, BLOCK, 0, 4, 4)
+        update(6 * BLOCK, BLOCK, 4, 4, 5)
+        last_delta(1)
+        quantize_delta(1, 7 * BLOCK, BLOCK, work[4][:].bitcast(BF16)[:, BANK : 2 * BANK])
+        for n in range(4):
+            update(7 * BLOCK, BLOCK, 2 * n, 2, (6, 7, 2, 3)[n])
+        finish(6 * BLOCK, BLOCK, 0, 4, True)
+        finish(6 * BLOCK, BLOCK, 4, 4, False)
+        for n in range(4):
+            finish(7 * BLOCK, BLOCK, 2 * n, 2, n % 2 == 0)

@@ -191,7 +191,7 @@ def tile_burstpropfeedbackdifferenceupdate_w8_kernel(tc, bt, b0, y_words, y_scal
 
         def finish(h0, width, i0, count, on_vector):
             bank = banks["update", h0, i0]
-            result = stream.tile([P, count, width], F32, name="result", bufs=6)
+            result = stream.tile([P, count, width], F32, name="result", bufs=10)
             if on_vector:
                 nc.vector.tensor_scalar(out=result[:], in0=bank[:], scalar1=1.0 / 32.0, scalar2=None, op0=ALU.mult)
             else:
@@ -212,10 +212,10 @@ def tile_burstpropfeedbackdifferenceupdate_w8_kernel(tc, bt, b0, y_words, y_scal
         for q in range(4):
             nc.scalar.dma_start(out=y_planes[32 * q : 32 * q + 4].bitcast(I32), in_=y_scales[:, 4 * q : 4 * q + 4, :].rearrange("g r n -> r g n").bitcast(I32))
         nc.scalar.activation(out=warm[:], in_=zeros[:, :2], func=ACT.Sigmoid)
+        load_x(0, 1)
         load_e(0)
         load_b(1)
         load_y(1)
-        load_x(0, 1)
         load_b(2)
         load_e(1)
         load_b(3)
@@ -238,9 +238,13 @@ def tile_burstpropfeedbackdifferenceupdate_w8_kernel(tc, bt, b0, y_words, y_scal
         widen_x(0, True)
         quantize_b(0, 2)
         widen_x(1, False)
+        widen_x(2, True)
+        widen_x(3, False)
         drives(0, 0, 0)
         drives(0, 1, 1)
+        warm_up(1)
         turn(1)
+        warm_up(1)
         empty_turn(1, stage_tile())
         drives(0, 2, 2)
         drives(0, 3, 3)
@@ -250,21 +254,21 @@ def tile_burstpropfeedbackdifferenceupdate_w8_kernel(tc, bt, b0, y_words, y_scal
             prob = stream.tile([P, 2, H], F32, name="prob")
             if t:
                 turn(2 * t + 1)
-                empty_turn(2 * t + 1, dp_region[t] if t > 1 else stage_tile())
+                empty_turn(2 * t + 1, dp_region[t] if t == 1 else stage_tile())
             for c in range(4):
                 gate(pre, c, t, c)
                 if t == 0 and c == 1:
-                    widen_x(2, True)
-                    widen_x(3, False)
+                    weave_x(0, 0, dp_region[0], "vector")
+                    quantize_b(1)
                     turn(2)
+                    drives(1, 0, 0)
+                    drives(1, 1, 1)
                 if c % 2 == 1:
                     sigmoid(prob, pre, (c - 1) * CHUNK, (c + 1) * CHUNK)
                 if t == 0 and c == 1:
-                    empty_turn(2, dp_region[0])
-                if t == 0:
-                    continue
+                    empty_turn(2, stage_tile())
                 if t < 3:
-                    if c == 1:
+                    if c == 1 and t:
                         drives(t + 1, 0, 0)
                         drives(t + 1, 1, 1)
                         turn(2 * t + 2)
@@ -273,28 +277,24 @@ def tile_burstpropfeedbackdifferenceupdate_w8_kernel(tc, bt, b0, y_words, y_scal
                 elif c < 2:
                     drives(PACK + c, 0, c)
             if 0 < t < 3:
-                empty_turn(2 * t + 2, stage_tile())
+                empty_turn(2 * t + 2, dp_region[t + 1])
             if t == 0:
-                quantize_b(1)
-                for c in range(4):
-                    drives(1, c, c)
-                weave_x(0, 0, stage_tile(), "vector")
+                weave_x(0, 1, stage_tile(), "vector")
+                quantize_x(0, 0)
                 quantize_b(2)
                 widen_x(4, False)
             elif t == 1:
-                weave_x(0, 1, dp_region[1], "vector")
-                quantize_x(0, 0)
+                widen_x(5, True)
                 quantize_b(3)
                 quantize_x(0, 1)
             elif t == 2:
-                widen_x(5, True)
-                quantize_b(4)
                 widen_x(6, True)
+                widen_x(7, True)
+                quantize_b(4)
                 quantize_b(5)
             else:
                 quantize_b(6)
                 drives(6, 0, 2)
-                widen_x(7, True)
                 quantize_b(7)
                 drives(7, 0, 3)
             if t < 3:
@@ -307,11 +307,11 @@ def tile_burstpropfeedbackdifferenceupdate_w8_kernel(tc, bt, b0, y_words, y_scal
         work = [kept("work%d" % c, [P, H], F32) for c in range(5)]
 
         def delta_first(b):
-            delta(0, b, dp_view[:, :, b * BLOCK : (b + 1) * BLOCK], work[b // 2][:].bitcast(BF16)[:, (b % 2) * BANK : (b % 2 + 1) * BANK])
+            delta(0, b, dp_view[:, :, b * BLOCK : (b + 1) * BLOCK], work[b // 2][:].bitcast(BF16)[:, (2 + b % 2) * BANK : (3 + b % 2) * BANK])
 
         def delta_second(b):
             dp = work[b // 2][:].rearrange("p (t h) -> p t h", t=PACK)[:, :, (b % 2) * BLOCK : (b % 2 + 1) * BLOCK]
-            delta(1, b, dp, work[b // 2 + 1][:].bitcast(BF16)[:, (2 + b % 2) * BANK : (3 + b % 2) * BANK])
+            delta(1, b, dp, work[b // 2 + 2][:].bitcast(BF16)[:, (b % 2) * BANK : (1 + b % 2) * BANK])
 
         modulation(0, 0, 4)
         modulation(0, 1, 5)
@@ -319,8 +319,13 @@ def tile_burstpropfeedbackdifferenceupdate_w8_kernel(tc, bt, b0, y_words, y_scal
             pre = stream.tile([P, 2, H], F32, name="pre")
             prob = stream.tile([P, 2, H], F32, name="prob")
             done = (c - 2) * CHUNK
-            if c < 2:
-                weave_x(1, c, stage_tile(), "scalar")
+            if c == 0:
+                woven_x = [stage_tile(), stage_tile()]
+                weave_x(1, 0, woven_x[0], "scalar", 0, CHUNK)
+            elif c == 1:
+                weave_x(1, 0, woven_x[0], "scalar", CHUNK, BANK)
+                weave_x(1, 1, woven_x[1], "scalar", 0, CHUNK)
+                weave_x(1, 1, woven_x[1], "gpsimd", CHUNK, BANK)
             else:
                 update(done, CHUNK, 0, 2, 6)
                 update(done, CHUNK, 2, 2, 7)
@@ -355,11 +360,12 @@ def tile_burstpropfeedbackdifferenceupdate_w8_kernel(tc, bt, b0, y_words, y_scal
                 modulation(0, 2 * c + 2 + a, 4 + a)
                 if a == 0:
                     drives(7, c + 1, 3)
-            if c < 2:
-                quantize_x(1, c)
-            quantize_delta(0, c * CHUNK, CHUNK, work[c][:].bitcast(BF16)[:, : 2 * BANK])
+            if c == 1:
+                quantize_x(1, 0)
+                quantize_x(1, 1)
+            quantize_delta(0, c * CHUNK, CHUNK, work[c][:].bitcast(BF16)[:, 2 * BANK :])
             if c:
-                quantize_delta(1, (c - 1) * CHUNK, CHUNK, work[c][:].bitcast(BF16)[:, 2 * BANK :])
+                quantize_delta(1, (c - 1) * CHUNK, CHUNK, work[c + 1][:].bitcast(BF16)[:, : 2 * BANK])
             difference(work[c], prob, nc.gpsimd, 0, H)
 
         pre = stream.tile([P, 2, H], F32, name="pre")
@@ -370,25 +376,22 @@ def tile_burstpropfeedbackdifferenceupdate_w8_kernel(tc, bt, b0, y_words, y_scal
         finish(done, CHUNK, 0, 2, False)
         finish(done, CHUNK, 2, 2, False)
         gate(pre, 0, 4, 3)
-        update(done, CHUNK, 4, 2, 0)
-        delta_first(6)
-        modulation(1, 4, 4)
         gate(pre, 1, 5, 3)
         sigmoid(prob, pre, 0, 2 * CHUNK)
-        update(done, CHUNK, 6, 2, 1)
-        delta_first(7)
-        modulation(1, 5, 5)
-        finish(done, CHUNK, 4, 2, False)
         gate(pre, 2, 6, 3)
-        modulation(1, 6, 2)
+        modulation(1, 4, 2)
         gate(pre, 3, 7, 3)
-        modulation(1, 7, 3)
+        modulation(1, 5, 3)
         sigmoid(prob, pre, 2 * CHUNK, H)
+        update(done, CHUNK, 4, 2, 0)
+        finish(done, CHUNK, 4, 2, False)
+        delta_first(6)
+        modulation(1, 6, 4)
+        update(done, CHUNK, 6, 2, 1)
         finish(done, CHUNK, 6, 2, False)
         delta_second(4)
         delta_second(5)
-        quantize_delta(0, 3 * CHUNK, CHUNK, work[3][:].bitcast(BF16)[:, : 2 * BANK])
-        quantize_delta(1, 2 * CHUNK, CHUNK, work[3][:].bitcast(BF16)[:, 2 * BANK :])
+        quantize_delta(1, 2 * CHUNK, CHUNK, work[4][:].bitcast(BF16)[:, : 2 * BANK])
         done = 2 * CHUNK
         dp_last = kept("dp_last", [P, PACK, CHUNK], F32)
         prob_view = prob[:].rearrange("p k (t h) -> p k t h", t=PACK)
@@ -398,24 +401,27 @@ def tile_burstpropfeedbackdifferenceupdate_w8_kernel(tc, bt, b0, y_words, y_scal
             engine.tensor_tensor(out=dp_last[:, :, cols], in0=prob_view[:, 0, :, cols], in1=prob_view[:, 1, :, cols], op=ALU.subtract)
 
         def last_delta(a):
-            delta(1, 6 + a, dp_last[:, :, a * BLOCK : (a + 1) * BLOCK], work[4][:].bitcast(BF16)[:, a * BANK : (a + 1) * BANK])
+            delta(1, 6 + a, dp_last[:, :, a * BLOCK : (a + 1) * BLOCK], work[4][:].bitcast(BF16)[:, (2 + a) * BANK : (3 + a) * BANK])
 
-        update(done, CHUNK, 0, 2, 6)
-        update(done, CHUNK, 2, 2, 7)
-        update(done, CHUNK, 4, 2, 0)
-        update(done, CHUNK, 6, 2, 1)
+        update(done, CHUNK, 0, 2, 2)
+        delta_first(7)
+        update(done, CHUNK, 2, 2, 3)
+        modulation(1, 7, 5)
+        update(done, CHUNK, 4, 2, 6)
+        update(done, CHUNK, 6, 2, 7)
         last_difference(nc.vector, 0)
-        last_difference(nc.vector, 1)
+        quantize_delta(0, 3 * CHUNK, CHUNK, work[3][:].bitcast(BF16)[:, 2 * BANK :])
         last_delta(0)
+        last_difference(nc.vector, 1)
         for i0 in range(0, TILES, 2):
             finish(done, CHUNK, i0, 2, False)
-        quantize_delta(1, 6 * BLOCK, BLOCK, work[4][:].bitcast(BF16)[:, :BANK])
-        update(6 * BLOCK, BLOCK, 0, 4, 4)
-        update(6 * BLOCK, BLOCK, 4, 4, 5)
+        quantize_delta(1, 6 * BLOCK, BLOCK, work[4][:].bitcast(BF16)[:, 2 * BANK : 3 * BANK])
+        update(6 * BLOCK, BLOCK, 0, 4, 0)
+        update(6 * BLOCK, BLOCK, 4, 4, 1)
         last_delta(1)
-        quantize_delta(1, 7 * BLOCK, BLOCK, work[4][:].bitcast(BF16)[:, BANK : 2 * BANK])
+        quantize_delta(1, 7 * BLOCK, BLOCK, work[4][:].bitcast(BF16)[:, 3 * BANK :])
         for n in range(4):
-            update(7 * BLOCK, BLOCK, 2 * n, 2, (6, 7, 2, 3)[n])
+            update(7 * BLOCK, BLOCK, 2 * n, 2, (4, 2, 3, 6)[n])
         finish(6 * BLOCK, BLOCK, 0, 4, True)
         finish(6 * BLOCK, BLOCK, 4, 4, False)
         for n in range(4):

@@ -4,7 +4,7 @@ import concourse.mybir as mybir
 from concourse.masks import make_identity
 
 N, C, H, D = 1024, 1024, 1024, 1024
-FLOPS = 3 * 2 * 1024 * 1024 * 1024
+FLOPS = 2 * N * C * H * 2 + 2 * N * D * H
 
 F32 = mybir.dt.float32
 BF16 = mybir.dt.bfloat16
@@ -20,10 +20,18 @@ P = 128
 PACK = 4
 PASSES = 2
 TILES = PASSES * PACK
+SIDES = 2
 BANK = 512
-CHUNK = 256
-BLOCK = 128
+CHUNK = BANK // SIDES
+CHUNKS = H // CHUNK
+STRIP = BANK // PACK
 RUN = 4
+OUT_SCALE = 1.0 / 32.0
+
+DRIVE_BANKS = (0, 1, 2, 3)
+TURN_BANKS = (4, 5, 6, 7)
+MOD_BANKS = (4, 5)
+OUT_BANKS = (6, 7)
 
 
 def tile_burstpropfeedbackdifferenceupdate_w8_kernel(tc, bt, b0, y_words, y_scales, e, x_bytes, x_scale, m, out):
@@ -38,24 +46,24 @@ def tile_burstpropfeedbackdifferenceupdate_w8_kernel(tc, bt, b0, y_words, y_scal
             return keep.tile(shape, dtype, name=name, align_bytes=64)
 
         identity = kept("identity", [P, P], F32)
-        y_planes = kept("y_planes", [P, PASSES, H], U8)
-        y_codes = [kept("y_codes%d" % i, [P, PASSES, H // 2], U32) for i in range(2)]
+        y_scale_rows = kept("y_scale_rows", [P, PASSES, H], U8)
+        y_codes = [kept("y_codes%d" % half, [P, PASSES, H // 2], U32) for half in range(2)]
         x_scale_sb = kept("x_scale_sb", [P, TILES], F32)
         m_sb = kept("m_sb", [P, TILES], BF16)
         m_diag = kept("m_diag", [P, TILES, P], BF16)
         e_first = [kept("e_first%d" % t, [P, H], BF16) for t in range(PACK)]
         e_second = kept("e_second", [P, PACK * H], BF16)
         e_rows = [e_first[t][:] for t in range(PACK)] + [e_second[:, t * H : (t + 1) * H] for t in range(PACK)]
-        x_raw = [kept("x_raw%d" % g, [P, 2 * D], U8) for g in range(2 * PASSES)]
+        x_raw = [kept("x_raw%d" % pair, [P, 2 * D], U8) for pair in range(TILES // 2)]
         x_wide = [kept("x_wide%d" % g, [P, PACK * D], BF16) for g in range(PASSES)]
         x_codes = [kept("x_codes%d" % g, [P, D], U32) for g in range(PASSES)]
-        x_planes = [kept("x_planes%d" % g, [P, D], U8) for g in range(PASSES)]
-        b_codes = [kept("b_codes%d" % j, [P, 2 * PASSES * P], U32) for j in range(TILES)]
-        b_planes = [kept("b_planes%d" % j, [P, 2 * PASSES * P], U8) for j in range(TILES)]
+        x_scale_rows = [kept("x_scale_rows%d" % g, [P, D], U8) for g in range(PASSES)]
+        b_codes = [kept("b_codes%d" % j, [P, SIDES * PASSES * P], U32) for j in range(TILES)]
+        b_scale_rows = [kept("b_scale_rows%d" % j, [P, SIDES * PASSES * P], U8) for j in range(TILES)]
         delta_codes = [kept("delta_codes%d" % g, [P, H], U32) for g in range(PASSES)]
-        delta_planes = [kept("delta_planes%d" % g, [P, H], U8) for g in range(PASSES)]
+        delta_scale_rows = [kept("delta_scale_rows%d" % g, [P, H], U8) for g in range(PASSES)]
         dp_first = kept("dp_first", [P, PACK * H], F32)
-        warm = kept("warm", [P, 2], F32)
+        table_probe = kept("table_probe", [P, 2], F32)
         zeros = kept("zeros", [P, BANK], BF16)
 
         b_rows = {}
@@ -65,52 +73,58 @@ def tile_burstpropfeedbackdifferenceupdate_w8_kernel(tc, bt, b0, y_words, y_scal
         def bank_tile(number, shape):
             return psum.tile(shape, F32, name="bank%d" % number)
 
-        def load_b(j):
-            g, t = divmod(j, PACK)
-            for k, src in enumerate((bt, b0)):
-                rows = stream.tile([P, C], BF16, name="b_rows", bufs=16, align_bytes=64)
-                nc.sync.dma_start(out=rows[:], in_=src.rearrange("(g p t) c -> g t p c", p=P, t=PACK)[g, t])
-                b_rows[j, k] = rows
-
-        def load_y(i):
-            words = y_words.rearrange("g p n t -> p g (n t)")[:, :, i * 2 * H : (i + 1) * 2 * H]
-            nc.sync.dma_start(out=y_codes[i][:].bitcast(I32), in_=words.bitcast(I32))
-
-        def load_e(t):
-            nc.sync.dma_start(out=e_first[t][:], in_=e.rearrange("(g p t) h -> g t p h", p=P, t=PACK)[0, t])
-
-        def load_x(g, a):
-            nc.sync.dma_start(out=x_raw[2 * g + a][:], in_=x_bytes.rearrange("(g p a t) d -> g a p (t d)", p=P, a=2, t=2)[g, a])
-
-        def turn(j):
-            for k in range(2):
-                words = b_rows[j, k][:].bitcast(F32)
-                bank = bank_tile(4 + 2 * (j % 2) + k, [P, PASSES, 2, P])
-                for g in range(PASSES):
-                    for u in range(2):
-                        nc.tensor.transpose(bank[:, g, u, :], words[:, 256 * g + u : 256 * (g + 1) : 2], identity[:])
-                banks["turn", j, k] = bank
-
         def stage_tile():
             tile = stream.tile([P, H], F32, name="stage", bufs=3, align_bytes=64)
             return tile[:]
 
-        def empty_turn(j, where, on_vector=()):
+        def load_b(j):
+            g, t = divmod(j, PACK)
+            for side, src in enumerate((bt, b0)):
+                rows = stream.tile([P, C], BF16, name="b_rows", bufs=SIDES * TILES, align_bytes=64)
+                nc.sync.dma_start(out=rows[:], in_=src.rearrange("(g p t) c -> g t p c", p=P, t=PACK)[g, t])
+                b_rows[j, side] = rows
+
+        def load_y(half):
+            words = y_words.rearrange("g p n t -> p g (n t)")[:, :, half * 2 * H : (half + 1) * 2 * H]
+            nc.sync.dma_start(out=y_codes[half][:].bitcast(I32), in_=words.bitcast(I32))
+
+        def load_e(t):
+            nc.sync.dma_start(out=e_first[t][:], in_=e.rearrange("(g p t) h -> g t p h", p=P, t=PACK)[0, t])
+
+        def load_x(pair):
+            rows = x_bytes.rearrange("(g p a t) d -> g a p (t d)", p=P, a=2, t=2)[pair // 2, pair % 2]
+            nc.sync.dma_start(out=x_raw[pair][:], in_=rows)
+
+        def warm_up(count):
+            bank = bank_tile(DRIVE_BANKS[-1], [P, BANK])
+            for n in range(count):
+                nc.tensor.matmul(bank[:], lhsT=zeros[:, :P], rhs=zeros[:], start=True, stop=True)
+
+        def turn(j):
+            for side in range(SIDES):
+                words = b_rows[j, side][:].bitcast(F32)
+                bank = bank_tile(TURN_BANKS[SIDES * (j % 2) + side], [P, PASSES, 2, P])
+                for g in range(PASSES):
+                    for u in range(2):
+                        nc.tensor.transpose(bank[:, g, u, :], words[:, 2 * P * g + u : 2 * P * (g + 1) : 2], identity[:])
+                banks["turn", j, side] = bank
+
+        def empty_turn(j, where):
             staged["b", j] = where
-            for k in range(2):
-                dst = where[:, k * BANK : (k + 1) * BANK].rearrange("p (g r u) -> p g r u", g=PASSES, u=2)
-                src = banks["turn", j, k][:].rearrange("p g u r -> p g r u")
-                if k not in on_vector:
-                    nc.scalar.copy(out=dst, in_=src)
-                else:
-                    nc.vector.tensor_copy(out=dst, in_=src)
+            for side in range(SIDES):
+                dst = where[:, side * BANK : (side + 1) * BANK].rearrange("p (g r u) -> p g r u", g=PASSES, u=2)
+                nc.scalar.copy(out=dst, in_=banks["turn", j, side][:].rearrange("p g u r -> p g r u"))
 
         def quantize_b(j, parts=1):
             src = staged["b", j].bitcast(BF16)
-            w = BANK // parts
-            for k in range(parts):
-                nc.vector.quantize_mx(out=b_codes[j][:, k * w : (k + 1) * w].bitcast(FP8X4), scales=b_planes[j][:, k * w : (k + 1) * w],
-                                      in_=src[:, 4 * k * w : 4 * (k + 1) * w])
+            width = SIDES * PASSES * P // parts
+            for part in range(parts):
+                cols = slice(part * width, (part + 1) * width)
+                nc.vector.quantize_mx(
+                    out=b_codes[j][:, cols].bitcast(FP8X4),
+                    scales=b_scale_rows[j][:, cols],
+                    in_=src[:, PACK * cols.start : PACK * cols.stop],
+                )
 
         def widen_x(j, on_vector):
             g, t = divmod(j, PACK)
@@ -121,308 +135,381 @@ def tile_burstpropfeedbackdifferenceupdate_w8_kernel(tc, bt, b0, y_words, y_scal
             else:
                 nc.scalar.activation(out=dst, in_=src, func=ACT.Copy, scale=x_scale_sb[:, j : j + 1])
 
-        def weave_x(g, half, where, engine, lo=0, hi=BANK):
+        def x_views(g, half, where, lo, hi):
             staged["x", g, half] = where
             src = x_wide[g][:].rearrange("p (t a d) -> p a t d", t=PACK, a=2)[:, half, :, lo:hi]
-            dst = where.bitcast(BF16)[:, PACK * lo : PACK * hi]
-            if engine == "gpsimd":
-                nc.gpsimd.tensor_scalar(out=dst.rearrange("p (d t) -> p d t", t=PACK), in0=src.rearrange("p t d -> p d t"), scalar1=1.0, scalar2=0.0, op0=ALU.mult, op1=ALU.add)
-                return
-            src = src.rearrange("p t (c i) -> p c t i", i=RUN)
-            dst = dst.rearrange("p (c i t) -> p c t i", t=PACK, i=RUN)
-            if engine == "vector":
-                nc.vector.tensor_copy(out=dst, in_=src)
-            else:
-                nc.scalar.copy(out=dst, in_=src)
+            return src, where.bitcast(BF16)[:, PACK * lo : PACK * hi]
+
+        def weave_x(copy, g, half, where, lo=0, hi=D // 2):
+            src, dst = x_views(g, half, where, lo, hi)
+            copy(out=dst.rearrange("p (c i t) -> p c t i", t=PACK, i=RUN), in_=src.rearrange("p t (c i) -> p c t i", i=RUN))
+
+        def weave_x_gpsimd(g, half, where, lo, hi):
+            src, dst = x_views(g, half, where, lo, hi)
+            nc.gpsimd.tensor_scalar(
+                out=dst.rearrange("p (d t) -> p d t", t=PACK),
+                in0=src.rearrange("p t d -> p d t"),
+                scalar1=1.0,
+                scalar2=0.0,
+                op0=ALU.mult,
+                op1=ALU.add,
+            )
 
         def quantize_x(g, half):
-            cols = slice(half * BANK, (half + 1) * BANK)
-            nc.vector.quantize_mx(out=x_codes[g][:, cols].bitcast(FP8X4), scales=x_planes[g][:, cols], in_=staged["x", g, half].bitcast(BF16))
-
-        def drive_group(dst, j, k, h0, width):
-            i, c0 = divmod(h0, H // 2)
-            for g in range(PASSES):
-                cols = slice((k * PASSES + g) * P, (k * PASSES + g + 1) * P)
-                nc.tensor.matmul_mx(out=dst, lhsT=b_codes[j][:, cols].bitcast(FP8X4), lhsT_scale=b_planes[j][:, cols],
-                                    rhs=y_codes[i][:, g, c0 : c0 + width].bitcast(FP8X4), rhs_scale=y_planes[:, g, h0 : h0 + width],
-                                    start=(g == 0), stop=(g == PASSES - 1))
+            cols = slice(half * D // 2, (half + 1) * D // 2)
+            nc.vector.quantize_mx(
+                out=x_codes[g][:, cols].bitcast(FP8X4), scales=x_scale_rows[g][:, cols], in_=staged["x", g, half].bitcast(BF16)
+            )
 
         def drives(j, c, number):
-            bank = bank_tile(number, [P, 2, CHUNK])
-            for k in range(2):
-                drive_group(bank[:, k, :], j, k, c * CHUNK, CHUNK)
+            bank = bank_tile(number, [P, SIDES, CHUNK])
+            half, c0 = divmod(c * CHUNK, H // 2)
+            for side in range(SIDES):
+                for g in range(PASSES):
+                    cols = slice((side * PASSES + g) * P, (side * PASSES + g + 1) * P)
+                    nc.tensor.matmul_mx(
+                        out=bank[:, side, :],
+                        lhsT=b_codes[j][:, cols].bitcast(FP8X4),
+                        lhsT_scale=b_scale_rows[j][:, cols],
+                        rhs=y_codes[half][:, g, c0 : c0 + CHUNK].bitcast(FP8X4),
+                        rhs_scale=y_scale_rows[:, g, c * CHUNK : (c + 1) * CHUNK],
+                        start=(g == 0),
+                        stop=(g == PASSES - 1),
+                    )
             banks["drive", j, c] = bank
 
-        def gate(pre, slot, j, c):
-            nc.vector.scalar_tensor_tensor(out=pre[:, :, slot * CHUNK : (slot + 1) * CHUNK], in0=e_rows[j][:, c * CHUNK : (c + 1) * CHUNK].unsqueeze(1).broadcast_to([P, 2, CHUNK]),
-                                           scalar=1.0, in1=banks["drive", j, c][:], op0=ALU.subtract, op1=ALU.mult)
+        def gate(pre, slot, j, h0, width):
+            c, c0 = divmod(h0, CHUNK)
+            nc.vector.scalar_tensor_tensor(
+                out=pre[:, :, slot * width : (slot + 1) * width],
+                in0=e_rows[j][:, h0 : h0 + width].unsqueeze(1).broadcast_to([P, SIDES, width]),
+                scalar=1.0,
+                in1=banks["drive", j, c][:, :, c0 : c0 + width],
+                op0=ALU.subtract,
+                op1=ALU.mult,
+            )
+
+        def step_tiles(width):
+            pre = stream.tile([P, SIDES, width], F32, name="pre")
+            prob = stream.tile([P, SIDES, width], F32, name="prob")
+            return pre, prob
 
         def sigmoid(prob, pre, lo, hi):
             nc.scalar.activation(out=prob[:, :, lo:hi], in_=pre[:, :, lo:hi], func=ACT.Sigmoid, scale=-4.0)
 
-        def difference(dst, prob, engine, lo, hi):
-            engine.tensor_tensor(out=dst[:, lo:hi], in0=prob[:, 0, lo:hi], in1=prob[:, 1, lo:hi], op=ALU.subtract)
+        def difference(engine, dp, prob, lo, hi):
+            engine.tensor_tensor(out=dp[:, lo:hi], in0=prob[:, 0, lo:hi], in1=prob[:, 1, lo:hi], op=ALU.subtract)
 
-        def warm_up(count):
-            bank = bank_tile(3, [P, BANK])
-            for n in range(count):
-                nc.tensor.matmul(bank[:], lhsT=zeros[:, :P], rhs=zeros[:], start=True, stop=True)
-
-        def modulation(g, b, number):
-            bank = bank_tile(number, [P, PACK, BLOCK])
+        def modulation(g, s, number):
+            bank = bank_tile(number, [P, PACK, STRIP])
             for t in range(PACK):
-                rows = e_rows[g * PACK + t][:, b * BLOCK : (b + 1) * BLOCK]
-                nc.tensor.matmul(bank[:, t, :], lhsT=m_diag[:, g * PACK + t, :], rhs=rows, start=True, stop=True)
-            banks["mod", g, b] = bank
+                j = g * PACK + t
+                nc.tensor.matmul(bank[:, t, :], lhsT=m_diag[:, j, :], rhs=e_rows[j][:, s * STRIP : (s + 1) * STRIP], start=True, stop=True)
+            banks["mod", g, s] = bank
 
-        def delta(g, b, dp, dst):
-            nc.vector.tensor_tensor(out=dst.rearrange("p (c i t) -> p c t i", t=PACK, i=RUN), in0=dp.rearrange("p t (c i) -> p c t i", i=RUN),
-                                    in1=banks["mod", g, b][:].rearrange("p t (c i) -> p c t i", i=RUN), op=ALU.mult)
+        def delta(g, s, dp, woven):
+            nc.vector.tensor_tensor(
+                out=woven.rearrange("p (c i t) -> p c t i", t=PACK, i=RUN),
+                in0=dp.rearrange("p t (c i) -> p c t i", i=RUN),
+                in1=banks["mod", g, s][:].rearrange("p t (c i) -> p c t i", i=RUN),
+                op=ALU.mult,
+            )
+
+        def quantize_delta(g, h0, width, woven):
+            cols = slice(h0, h0 + width)
+            nc.vector.quantize_mx(out=delta_codes[g][:, cols].bitcast(FP8X4), scales=delta_scale_rows[g][:, cols], in_=woven)
 
         def update(h0, width, i0, count, number):
             bank = bank_tile(number, [P, count, width])
-            for u in range(count):
-                cols = slice((i0 + u) * P, (i0 + u + 1) * P)
+            for i in range(count):
+                rows = slice((i0 + i) * P, (i0 + i + 1) * P)
                 for g in range(PASSES):
-                    nc.tensor.matmul_mx(out=bank[:, u, :], lhsT=x_codes[g][:, cols].bitcast(FP8X4), lhsT_scale=x_planes[g][:, cols],
-                                        rhs=delta_codes[g][:, h0 : h0 + width].bitcast(FP8X4), rhs_scale=delta_planes[g][:, h0 : h0 + width],
-                                        start=(g == 0), stop=(g == PASSES - 1))
+                    nc.tensor.matmul_mx(
+                        out=bank[:, i, :],
+                        lhsT=x_codes[g][:, rows].bitcast(FP8X4),
+                        lhsT_scale=x_scale_rows[g][:, rows],
+                        rhs=delta_codes[g][:, h0 : h0 + width].bitcast(FP8X4),
+                        rhs_scale=delta_scale_rows[g][:, h0 : h0 + width],
+                        start=(g == 0),
+                        stop=(g == PASSES - 1),
+                    )
             banks["update", h0, i0] = bank
 
-        def finish(h0, width, i0, count, on_vector):
-            bank = banks["update", h0, i0]
+        def finish(h0, width, i0, count, on_vector=False):
             result = stream.tile([P, count, width], F32, name="result", bufs=10)
+            bank = banks["update", h0, i0]
             if on_vector:
-                nc.vector.tensor_scalar(out=result[:], in0=bank[:], scalar1=1.0 / 32.0, scalar2=None, op0=ALU.mult)
+                nc.vector.tensor_scalar(out=result[:], in0=bank[:], scalar1=OUT_SCALE, scalar2=None, op0=ALU.mult)
             else:
-                nc.scalar.activation(out=result[:], in_=bank[:], func=ACT.Copy, scale=1.0 / 32.0)
-            nc.sync.dma_start(out=out.rearrange("(i p) h -> p i h", p=P)[:, i0 : i0 + count, h0 : h0 + width], in_=result[:])
+                nc.scalar.activation(out=result[:], in_=bank[:], func=ACT.Copy, scale=OUT_SCALE)
+            rows = out.rearrange("(i p) h -> p i h", p=P)[:, i0 : i0 + count, h0 : h0 + width]
+            nc.sync.dma_start(out=rows, in_=result[:])
 
-        def quantize_delta(g, h0, width, src):
-            nc.vector.quantize_mx(out=delta_codes[g][:, h0 : h0 + width].bitcast(FP8X4), scales=delta_planes[g][:, h0 : h0 + width], in_=src)
+        def update_pair(c, first, numbers):
+            for n, number in enumerate(numbers):
+                update(c * CHUNK, CHUNK, first + 2 * n, 2, number)
+
+        def finish_pair(c, first):
+            for n in range(2):
+                finish(c * CHUNK, CHUNK, first + 2 * n, 2)
 
         nc.gpsimd.dma_start(out=m_sb[:].rearrange("p (g t) -> p g t", t=PACK), in_=m.rearrange("(g p t) -> p g t", p=P, t=PACK))
-        nc.gpsimd.dma_start(out=x_scale_sb[:].rearrange("p (g t) -> p g t", t=PACK), in_=x_scale.rearrange("(g p t) o -> p g (t o)", p=P, t=PACK))
+        nc.gpsimd.dma_start(
+            out=x_scale_sb[:].rearrange("p (g t) -> p g t", t=PACK), in_=x_scale.rearrange("(g p t) o -> p g (t o)", p=P, t=PACK)
+        )
         make_identity(nc, identity[:])
-        nc.vector.memset(y_planes[:].rearrange("p g n -> p (g n)").bitcast(I32), 0)
         nc.vector.memset(zeros[:], 0.0)
+        nc.vector.memset(y_scale_rows[:].rearrange("p g n -> p (g n)").bitcast(I32), 0)
         load_b(0)
-        load_x(0, 0)
+        load_x(0)
         load_y(0)
-        for q in range(4):
-            nc.scalar.dma_start(out=y_planes[32 * q : 32 * q + 4].bitcast(I32), in_=y_scales[:, 4 * q : 4 * q + 4, :].rearrange("g r n -> r g n").bitcast(I32))
-        nc.scalar.activation(out=warm[:], in_=zeros[:, :2], func=ACT.Sigmoid)
-        load_x(0, 1)
+        for quadrant in range(4):
+            nc.scalar.dma_start(
+                out=y_scale_rows[32 * quadrant : 32 * quadrant + 4].bitcast(I32),
+                in_=y_scales[:, 4 * quadrant : 4 * quadrant + 4, :].rearrange("g r n -> r g n").bitcast(I32),
+            )
+        nc.scalar.activation(out=table_probe[:], in_=zeros[:, :2], func=ACT.Sigmoid)
+        load_x(1)
         load_e(0)
         load_b(1)
         load_y(1)
-        load_b(2)
-        load_e(1)
-        load_b(3)
-        load_x(1, 0)
-        load_b(4)
-        load_e(2)
-        load_b(5)
-        load_x(1, 1)
-        load_b(6)
-        load_e(3)
-        load_b(7)
+        for t in range(1, PACK):
+            load_b(2 * t)
+            load_e(t)
+            load_b(2 * t + 1)
+            if t < PACK - 1:
+                load_x(t + 1)
         nc.sync.dma_start(out=e_second[:], in_=e.rearrange("(g p t) h -> g p (t h)", p=P, t=PACK)[1])
 
-        dp_region = [dp_first[:, t * H : (t + 1) * H] for t in range(PACK)]
-        nc.vector.tensor_tensor(out=m_diag[:], in0=identity[:].unsqueeze(1).broadcast_to([P, TILES, P]), in1=m_sb[:].unsqueeze(2).broadcast_to([P, TILES, P]), op=ALU.mult)
-        warm_up(4)
+        nc.vector.tensor_tensor(
+            out=m_diag[:],
+            in0=identity[:].unsqueeze(1).broadcast_to([P, TILES, P]),
+            in1=m_sb[:].unsqueeze(2).broadcast_to([P, TILES, P]),
+            op=ALU.mult,
+        )
+        warm_up(3)
         turn(0)
         warm_up(3)
         empty_turn(0, stage_tile())
-        widen_x(0, True)
-        quantize_b(0, 2)
-        widen_x(1, False)
-        widen_x(2, True)
-        widen_x(3, False)
-        drives(0, 0, 0)
-        drives(0, 1, 1)
-        warm_up(1)
+        widen_x(0, on_vector=True)
+        quantize_b(0, parts=SIDES)
+        widen_x(1, on_vector=False)
+        widen_x(2, on_vector=True)
+        widen_x(3, on_vector=False)
+        drives(0, 0, DRIVE_BANKS[0])
+        drives(0, 1, DRIVE_BANKS[1])
         turn(1)
         warm_up(1)
         empty_turn(1, stage_tile())
-        drives(0, 2, 2)
-        drives(0, 3, 3)
+        drives(0, 2, DRIVE_BANKS[2])
+        drives(0, 3, DRIVE_BANKS[3])
 
-        for t in range(PACK):
-            pre = stream.tile([P, 2, H], F32, name="pre")
-            prob = stream.tile([P, 2, H], F32, name="prob")
-            if t:
-                turn(2 * t + 1)
-                empty_turn(2 * t + 1, dp_region[t] if t == 1 else stage_tile())
-            for c in range(4):
-                gate(pre, c, t, c)
-                if t == 0 and c == 1:
-                    weave_x(0, 0, dp_region[0], "vector")
-                    quantize_b(1)
-                    turn(2)
-                    drives(1, 0, 0)
-                    drives(1, 1, 1)
+        dp_part = [dp_first[:, t * H : (t + 1) * H] for t in range(PACK)]
+
+        pre, prob = step_tiles(H)
+        gate(pre, 0, 0, 0, CHUNK)
+        gate(pre, 1, 0, CHUNK, CHUNK)
+        weave_x(nc.vector.tensor_copy, 0, 0, dp_part[0])
+        quantize_b(1)
+        turn(2)
+        drives(1, 0, DRIVE_BANKS[0])
+        drives(1, 1, DRIVE_BANKS[1])
+        sigmoid(prob, pre, 0, H // 2)
+        empty_turn(2, stage_tile())
+        for c in range(2, CHUNKS):
+            gate(pre, c, 0, c * CHUNK, CHUNK)
+            if c == CHUNKS - 1:
+                sigmoid(prob, pre, H // 2, H)
+            drives(1, c, DRIVE_BANKS[c])
+        weave_x(nc.vector.tensor_copy, 0, 1, stage_tile())
+        quantize_x(0, 0)
+        quantize_b(2)
+        widen_x(4, on_vector=False)
+        difference(nc.gpsimd, dp_part[0], prob, 0, H)
+
+        def first_pass_gates(t, where):
+            pre, prob = step_tiles(H)
+            turn(2 * t + 1)
+            empty_turn(2 * t + 1, where)
+            for c in range(CHUNKS):
+                gate(pre, c, t, c * CHUNK, CHUNK)
                 if c % 2 == 1:
                     sigmoid(prob, pre, (c - 1) * CHUNK, (c + 1) * CHUNK)
-                if t == 0 and c == 1:
-                    empty_turn(2, stage_tile())
-                if t < 3:
-                    if c == 1 and t:
-                        drives(t + 1, 0, 0)
-                        drives(t + 1, 1, 1)
-                        turn(2 * t + 2)
-                    if c >= 2:
-                        drives(t + 1, c, c)
-                elif c < 2:
-                    drives(PACK + c, 0, c)
-            if 0 < t < 3:
-                empty_turn(2 * t + 2, dp_region[t + 1])
-            if t == 0:
-                weave_x(0, 1, stage_tile(), "vector")
-                quantize_x(0, 0)
-                quantize_b(2)
-                widen_x(4, False)
-            elif t == 1:
-                widen_x(5, True)
-                quantize_b(3)
-                quantize_x(0, 1)
-            elif t == 2:
-                widen_x(6, True)
-                widen_x(7, True)
-                quantize_b(4)
-                quantize_b(5)
-            else:
-                quantize_b(6)
-                drives(6, 0, 2)
-                quantize_b(7)
-                drives(7, 0, 3)
-            if t < 3:
-                difference(dp_region[t], prob, nc.gpsimd, 0, H)
-            else:
-                difference(dp_region[t], prob, nc.gpsimd, 0, CHUNK)
-                difference(dp_region[t], prob, nc.gpsimd, CHUNK, H)
+                if t == PACK - 1:
+                    if c < 2:
+                        drives(PACK + c, 0, DRIVE_BANKS[c])
+                elif c == 1:
+                    drives(t + 1, 0, DRIVE_BANKS[0])
+                    drives(t + 1, 1, DRIVE_BANKS[1])
+                    turn(2 * t + 2)
+                elif c > 1:
+                    drives(t + 1, c, DRIVE_BANKS[c])
+            if t < PACK - 1:
+                empty_turn(2 * t + 2, dp_part[t + 1])
+            return prob
 
-        dp_view = dp_first[:].rearrange("p (t h) -> p t h", t=PACK)
-        work = [kept("work%d" % c, [P, H], F32) for c in range(5)]
+        prob = first_pass_gates(1, dp_part[1])
+        widen_x(5, on_vector=True)
+        quantize_b(3)
+        quantize_x(0, 1)
+        difference(nc.gpsimd, dp_part[1], prob, 0, H)
 
-        def delta_first(b):
-            delta(0, b, dp_view[:, :, b * BLOCK : (b + 1) * BLOCK], work[b // 2][:].bitcast(BF16)[:, (2 + b % 2) * BANK : (3 + b % 2) * BANK])
+        prob = first_pass_gates(2, stage_tile())
+        widen_x(6, on_vector=True)
+        widen_x(7, on_vector=True)
+        quantize_b(4)
+        quantize_b(5)
+        difference(nc.gpsimd, dp_part[2], prob, 0, H)
 
-        def delta_second(b):
-            dp = work[b // 2][:].rearrange("p (t h) -> p t h", t=PACK)[:, :, (b % 2) * BLOCK : (b % 2 + 1) * BLOCK]
-            delta(1, b, dp, work[b // 2 + 2][:].bitcast(BF16)[:, (b % 2) * BANK : (1 + b % 2) * BANK])
+        prob = first_pass_gates(3, stage_tile())
+        for t in range(2, PACK):
+            quantize_b(PACK + t)
+            drives(PACK + t, 0, DRIVE_BANKS[t])
+        difference(nc.gpsimd, dp_part[3], prob, 0, CHUNK)
+        difference(nc.gpsimd, dp_part[3], prob, CHUNK, H)
 
-        modulation(0, 0, 4)
-        modulation(0, 1, 5)
-        for c in range(3):
-            pre = stream.tile([P, 2, H], F32, name="pre")
-            prob = stream.tile([P, 2, H], F32, name="prob")
-            done = (c - 2) * CHUNK
-            if c == 0:
-                woven_x = [stage_tile(), stage_tile()]
-                weave_x(1, 0, woven_x[0], "scalar", 0, CHUNK)
-            elif c == 1:
-                weave_x(1, 0, woven_x[0], "scalar", CHUNK, BANK)
-                weave_x(1, 1, woven_x[1], "scalar", 0, CHUNK)
-                weave_x(1, 1, woven_x[1], "gpsimd", CHUNK, BANK)
-            else:
-                update(done, CHUNK, 0, 2, 6)
-                update(done, CHUNK, 2, 2, 7)
-                finish(done, CHUNK, 0, 2, False)
-                finish(done, CHUNK, 2, 2, False)
-            gate(pre, 0, 4, c)
-            drives(4, c + 1, 0)
-            if c:
-                delta_first(2 * c)
-                modulation(1, 2 * c - 2, 4)
-            gate(pre, 1, 5, c)
-            sigmoid(prob, pre, 0, 2 * CHUNK)
-            drives(5, c + 1, 1)
-            if c:
-                delta_first(2 * c + 1)
-                modulation(1, 2 * c - 1, 5)
-            if c >= 2:
-                update(done, CHUNK, 4, 2, 6)
-                update(done, CHUNK, 6, 2, 7)
-            gate(pre, 2, 6, c)
-            drives(6, c + 1, 2)
-            gate(pre, 3, 7, c)
-            sigmoid(prob, pre, 2 * CHUNK, H)
-            if c >= 2:
-                finish(done, CHUNK, 4, 2, False)
-                finish(done, CHUNK, 6, 2, False)
-            for a in range(2):
-                if c:
-                    delta_second(2 * c - 2 + a)
-                else:
-                    delta_first(a)
-                modulation(0, 2 * c + 2 + a, 4 + a)
-                if a == 0:
-                    drives(7, c + 1, 3)
-            if c == 1:
-                quantize_x(1, 0)
-                quantize_x(1, 1)
-            quantize_delta(0, c * CHUNK, CHUNK, work[c][:].bitcast(BF16)[:, 2 * BANK :])
-            if c:
-                quantize_delta(1, (c - 1) * CHUNK, CHUNK, work[c + 1][:].bitcast(BF16)[:, : 2 * BANK])
-            difference(work[c], prob, nc.gpsimd, 0, H)
+        dp_tiles = dp_first[:].rearrange("p (t h) -> p t h", t=PACK)
+        work = [kept("work%d" % c, [P, H], F32) for c in range(CHUNKS + 1)]
 
-        pre = stream.tile([P, 2, H], F32, name="pre")
-        prob = stream.tile([P, 2, H], F32, name="prob")
-        done = CHUNK
-        update(done, CHUNK, 0, 2, 6)
-        update(done, CHUNK, 2, 2, 7)
-        finish(done, CHUNK, 0, 2, False)
-        finish(done, CHUNK, 2, 2, False)
-        gate(pre, 0, 4, 3)
-        gate(pre, 1, 5, 3)
-        sigmoid(prob, pre, 0, 2 * CHUNK)
-        gate(pre, 2, 6, 3)
-        modulation(1, 4, 2)
-        gate(pre, 3, 7, 3)
-        modulation(1, 5, 3)
-        sigmoid(prob, pre, 2 * CHUNK, H)
-        update(done, CHUNK, 4, 2, 0)
-        finish(done, CHUNK, 4, 2, False)
-        delta_first(6)
-        modulation(1, 6, 4)
-        update(done, CHUNK, 6, 2, 1)
-        finish(done, CHUNK, 6, 2, False)
-        delta_second(4)
-        delta_second(5)
-        quantize_delta(1, 2 * CHUNK, CHUNK, work[4][:].bitcast(BF16)[:, : 2 * BANK])
-        done = 2 * CHUNK
-        dp_last = kept("dp_last", [P, PACK, CHUNK], F32)
-        prob_view = prob[:].rearrange("p k (t h) -> p k t h", t=PACK)
+        def woven_first(c):
+            return work[c][:].bitcast(BF16)[:, PACK * CHUNK :]
 
-        def last_difference(engine, a):
-            cols = slice(a * BLOCK, (a + 1) * BLOCK)
-            engine.tensor_tensor(out=dp_last[:, :, cols], in0=prob_view[:, 0, :, cols], in1=prob_view[:, 1, :, cols], op=ALU.subtract)
+        def woven_second(c):
+            return work[c + 2][:].bitcast(BF16)[:, : PACK * CHUNK]
 
-        def last_delta(a):
-            delta(1, 6 + a, dp_last[:, :, a * BLOCK : (a + 1) * BLOCK], work[4][:].bitcast(BF16)[:, (2 + a) * BANK : (3 + a) * BANK])
+        def delta_first(s):
+            c, a = divmod(s, 2)
+            delta(0, s, dp_tiles[:, :, s * STRIP : (s + 1) * STRIP], woven_first(c)[:, a * BANK : (a + 1) * BANK])
 
-        update(done, CHUNK, 0, 2, 2)
-        delta_first(7)
-        update(done, CHUNK, 2, 2, 3)
-        modulation(1, 7, 5)
-        update(done, CHUNK, 4, 2, 6)
-        update(done, CHUNK, 6, 2, 7)
-        last_difference(nc.vector, 0)
-        quantize_delta(0, 3 * CHUNK, CHUNK, work[3][:].bitcast(BF16)[:, 2 * BANK :])
-        last_delta(0)
-        last_difference(nc.vector, 1)
-        for i0 in range(0, TILES, 2):
-            finish(done, CHUNK, i0, 2, False)
-        quantize_delta(1, 6 * BLOCK, BLOCK, work[4][:].bitcast(BF16)[:, 2 * BANK : 3 * BANK])
-        update(6 * BLOCK, BLOCK, 0, 4, 0)
-        update(6 * BLOCK, BLOCK, 4, 4, 1)
-        last_delta(1)
-        quantize_delta(1, 7 * BLOCK, BLOCK, work[4][:].bitcast(BF16)[:, 3 * BANK :])
+        def delta_second(s):
+            c, a = divmod(s, 2)
+            dp = work[c][:].rearrange("p (t h) -> p t h", t=PACK)[:, :, a * STRIP : (a + 1) * STRIP]
+            delta(1, s, dp, woven_second(c)[:, a * BANK : (a + 1) * BANK])
+
+        def gate_second(pre, t, c):
+            gate(pre, t, PACK + t, c * CHUNK, CHUNK)
+
+        def drives_second(t, c):
+            drives(PACK + t, c, DRIVE_BANKS[t])
+
+        quarter = D // 4
+        modulation(0, 0, MOD_BANKS[0])
+        modulation(0, 1, MOD_BANKS[1])
+        pre, prob = step_tiles(H)
+        woven_x = [stage_tile(), stage_tile()]
+        weave_x(nc.scalar.copy, 1, 0, woven_x[0], 0, quarter)
+        for t in range(PACK):
+            gate_second(pre, t, 0)
+            if t % 2 == 1:
+                sigmoid(prob, pre, (t - 1) * CHUNK, (t + 1) * CHUNK)
+            if t < PACK - 1:
+                drives_second(t, 1)
+        delta_first(0)
+        modulation(0, 2, MOD_BANKS[0])
+        drives_second(PACK - 1, 1)
+        delta_first(1)
+        modulation(0, 3, MOD_BANKS[1])
+
+        def second_pass_rest(c, pre, prob, next_mods, updating):
+            drives_second(0, c + 1)
+            delta_first(2 * c)
+            modulation(1, 2 * c - 2, MOD_BANKS[0])
+            gate_second(pre, 1, c)
+            sigmoid(prob, pre, 0, H // 2)
+            drives_second(1, c + 1)
+            delta_first(2 * c + 1)
+            modulation(1, 2 * c - 1, MOD_BANKS[1])
+            if updating:
+                update_pair(c - 2, PACK, OUT_BANKS)
+            gate_second(pre, 2, c)
+            drives_second(2, c + 1)
+            gate_second(pre, 3, c)
+            sigmoid(prob, pre, H // 2, H)
+            if updating:
+                finish_pair(c - 2, PACK)
+            delta_second(2 * c - 2)
+            modulation(*next_mods[0], MOD_BANKS[0])
+            drives_second(3, c + 1)
+            delta_second(2 * c - 1)
+            modulation(*next_mods[1], MOD_BANKS[1])
+
+        def second_pass_end(c, prob):
+            quantize_delta(0, c * CHUNK, CHUNK, woven_first(c))
+            quantize_delta(1, (c - 1) * CHUNK, CHUNK, woven_second(c - 1))
+            difference(nc.gpsimd, work[c], prob, 0, H)
+
+        prob_before = prob
+        pre, prob = step_tiles(H)
+        weave_x(nc.scalar.copy, 1, 0, woven_x[0], quarter, 2 * quarter)
+        weave_x(nc.scalar.copy, 1, 1, woven_x[1], 0, quarter)
+        gate_second(pre, 0, 1)
+        quantize_delta(0, 0, CHUNK, woven_first(0))
+        difference(nc.gpsimd, work[0], prob_before, 0, H)
+        weave_x_gpsimd(1, 1, woven_x[1], quarter, 2 * quarter)
+        second_pass_rest(1, pre, prob, [(0, 4), (0, 5)], updating=False)
+        quantize_x(1, 0)
+        quantize_x(1, 1)
+        second_pass_end(1, prob)
+
+        pre, prob = step_tiles(H)
+        update_pair(0, 0, OUT_BANKS)
+        finish_pair(0, 0)
+        gate_second(pre, 0, 2)
+        second_pass_rest(2, pre, prob, [(0, 6), (1, 4)], updating=True)
+        second_pass_end(2, prob)
+
+        near, last = 2 * CHUNKS - 2, 2 * CHUNKS - 1
+        pre_near, prob_near = step_tiles(BANK)
+        pre_last, prob_last = step_tiles(BANK)
+        dp_strips = kept("dp_strips", [P, 2, BANK], F32)
+        woven_strips = work[CHUNKS][:].bitcast(BF16)[:, PACK * CHUNK :].rearrange("p (a w) -> p a w", a=2)
+
+        def gate_strip(pre, t, s):
+            gate(pre, t, PACK + t, s * STRIP, STRIP)
+
+        def delta_strip(s):
+            a = s - near
+            delta(1, s, dp_strips[:, a, :].rearrange("p (t h) -> p t h", t=PACK), woven_strips[:, a, :])
+
+        update_pair(1, 0, OUT_BANKS)
+        for t in range(PACK):
+            gate_strip(pre_near, t, near)
+            if t % 2 == 1:
+                sigmoid(prob_near, pre_near, (t - 1) * STRIP, (t + 1) * STRIP)
+        difference(nc.gpsimd, dp_strips[:, 0, :], prob_near, 0, BANK)
+        finish_pair(1, 0)
+        delta_first(near)
+        modulation(1, near - 1, MOD_BANKS[0])
+        gate_strip(pre_last, 0, last)
+        gate_strip(pre_last, 1, last)
+        sigmoid(prob_last, pre_last, 0, BANK // 2)
+        update_pair(1, PACK, DRIVE_BANKS[:2])
+        finish_pair(1, PACK)
+        delta_second(near - 2)
+        modulation(1, near, MOD_BANKS[1])
+        delta_second(near - 1)
+        modulation(0, last, MOD_BANKS[0])
+        gate_strip(pre_last, 2, last)
+        quantize_delta(1, 2 * CHUNK, CHUNK, woven_second(2))
+        gate_strip(pre_last, 3, last)
+        sigmoid(prob_last, pre_last, BANK // 2, BANK)
+        update_pair(2, 0, OUT_BANKS)
+        delta_strip(near)
+        modulation(1, last, MOD_BANKS[1])
+        update_pair(2, PACK, DRIVE_BANKS[2:])
+        finish_pair(2, 0)
+        finish_pair(2, PACK)
+        delta_first(last)
+        quantize_delta(1, near * STRIP, STRIP, woven_strips[:, 0, :])
+        quantize_delta(0, 3 * CHUNK, CHUNK, woven_first(3))
+        for n in range(2):
+            update(near * STRIP, STRIP, PACK * n, PACK, DRIVE_BANKS[n])
+        difference(nc.vector, dp_strips[:, 1, :], prob_last, 0, BANK)
+        delta_strip(last)
+        quantize_delta(1, last * STRIP, STRIP, woven_strips[:, 1, :])
+        for n, number in enumerate((MOD_BANKS[0], OUT_BANKS[0], OUT_BANKS[1], DRIVE_BANKS[2])):
+            update(last * STRIP, STRIP, 2 * n, 2, number)
+        for n in range(2):
+            finish(near * STRIP, STRIP, PACK * n, PACK, on_vector=(n == 1))
         for n in range(4):
-            update(7 * BLOCK, BLOCK, 2 * n, 2, (4, 2, 3, 6)[n])
-        finish(6 * BLOCK, BLOCK, 0, 4, True)
-        finish(6 * BLOCK, BLOCK, 4, 4, False)
-        for n in range(4):
-            finish(7 * BLOCK, BLOCK, 2 * n, 2, n % 2 == 0)
+            finish(last * STRIP, STRIP, 2 * n, 2, on_vector=(n % 2 == 1))

from contextlib import ExitStack

import concourse.mybir as mybir
from concourse.masks import make_identity

N, C, H, D = 1024, 1024, 1024, 1024
FLOPS = 2 * N * C * H * 2 + 2 * N * D * H

F32 = mybir.dt.float32
BF16 = mybir.dt.bfloat16
I32 = mybir.dt.int32
U32 = mybir.dt.uint32
U8 = mybir.dt.uint8
FP8 = mybir.dt.float8_e4m3fn
FP8X4 = mybir.dt.float8_e4m3fn_x4
ALU = mybir.AluOpType
ACT = mybir.ActivationFunctionType

P = 128
PACK = 4
PASSES = 2
TILES = PASSES * PACK
SIDES = 2
BANK = 512
CHUNK = BANK // SIDES
CHUNKS = H // CHUNK
STRIP = BANK // PACK
RUN = 4
OUT_SCALE = 1.0 / 32.0

DRIVE_BANKS = (0, 1, 2, 3)
TURN_BANKS = (4, 5, 6, 7)
MOD_BANKS = (4, 5)
OUT_BANKS = (6, 7)


def tile_burstpropfeedbackdifferenceupdate_w8_kernel(tc, bt, b0, y_words, y_scales, e, x_bytes, x_scale, m, out):
    nc = tc.nc
    with ExitStack() as ctx:
        keep = ctx.enter_context(tc.tile_pool(name="keep", bufs=1))
        stream = ctx.enter_context(tc.tile_pool(name="stream", bufs=2))
        psum = ctx.enter_context(tc.psum_pool(name="psum", bufs=1))
        ctx.enter_context(tc.manual_schedule())

        def kept(name, shape, dtype):
            return keep.tile(shape, dtype, name=name, align_bytes=64)

        identity = kept("identity", [P, P], F32)
        y_scale_rows = kept("y_scale_rows", [P, PASSES, H], U8)
        y_codes = [kept("y_codes%d" % half, [P, PASSES, H // 2], U32) for half in range(2)]
        x_scale_sb = kept("x_scale_sb", [P, TILES], F32)
        m_sb = kept("m_sb", [P, TILES], BF16)
        m_diag = kept("m_diag", [P, TILES, P], BF16)
        e_first = [kept("e_first%d" % t, [P, H], BF16) for t in range(PACK)]
        e_second = kept("e_second", [P, PACK * H], BF16)
        e_rows = [e_first[t][:] for t in range(PACK)] + [e_second[:, t * H : (t + 1) * H] for t in range(PACK)]
        x_raw = [kept("x_raw%d" % pair, [P, 2 * D], U8) for pair in range(TILES // 2)]
        x_wide = [kept("x_wide%d" % g, [P, PACK * D], BF16) for g in range(PASSES)]
        x_codes = [kept("x_codes%d" % g, [P, D], U32) for g in range(PASSES)]
        x_scale_rows = [kept("x_scale_rows%d" % g, [P, D], U8) for g in range(PASSES)]
        b_codes = [kept("b_codes%d" % j, [P, SIDES * PASSES * P], U32) for j in range(TILES)]
        b_scale_rows = [kept("b_scale_rows%d" % j, [P, SIDES * PASSES * P], U8) for j in range(TILES)]
        delta_codes = [kept("delta_codes%d" % g, [P, H], U32) for g in range(PASSES)]
        delta_scale_rows = [kept("delta_scale_rows%d" % g, [P, H], U8) for g in range(PASSES)]
        dp_first = kept("dp_first", [P, PACK * H], F32)
        table_probe = kept("table_probe", [P, 2], F32)
        zeros = kept("zeros", [P, BANK], BF16)

        b_rows = {}
        banks = {}
        staged = {}

        def bank_tile(number, shape):
            return psum.tile(shape, F32, name="bank%d" % number)

        def stage_tile():
            tile = stream.tile([P, H], F32, name="stage", bufs=3, align_bytes=64)
            return tile[:]

        def load_b(j):
            g, t = divmod(j, PACK)
            for side, src in enumerate((bt, b0)):
                rows = stream.tile([P, C], BF16, name="b_rows", bufs=SIDES * TILES, align_bytes=64)
                nc.sync.dma_start(out=rows[:], in_=src.rearrange("(g p t) c -> g t p c", p=P, t=PACK)[g, t])
                b_rows[j, side] = rows

        def load_y(half):
            words = y_words.rearrange("g p n t -> p g (n t)")[:, :, half * 2 * H : (half + 1) * 2 * H]
            nc.sync.dma_start(out=y_codes[half][:].bitcast(I32), in_=words.bitcast(I32))

        def load_e(t):
            nc.sync.dma_start(out=e_first[t][:], in_=e.rearrange("(g p t) h -> g t p h", p=P, t=PACK)[0, t])

        def load_x(pair):
            rows = x_bytes.rearrange("(g p a t) d -> g a p (t d)", p=P, a=2, t=2)[pair // 2, pair % 2]
            nc.sync.dma_start(out=x_raw[pair][:], in_=rows)

        def warm_up(count):
            bank = bank_tile(DRIVE_BANKS[-1], [P, BANK])
            for n in range(count):
                nc.tensor.matmul(bank[:], lhsT=zeros[:, :P], rhs=zeros[:], start=True, stop=True)

        def turn(j):
            for side in range(SIDES):
                words = b_rows[j, side][:].bitcast(F32)
                bank = bank_tile(TURN_BANKS[SIDES * (j % 2) + side], [P, PASSES, 2, P])
                for g in range(PASSES):
                    for u in range(2):
                        nc.tensor.transpose(bank[:, g, u, :], words[:, 2 * P * g + u : 2 * P * (g + 1) : 2], identity[:])
                banks["turn", j, side] = bank

        def empty_turn(j, where):
            staged["b", j] = where
            for side in range(SIDES):
                dst = where[:, side * BANK : (side + 1) * BANK].rearrange("p (g r u) -> p g r u", g=PASSES, u=2)
                nc.scalar.copy(out=dst, in_=banks["turn", j, side][:].rearrange("p g u r -> p g r u"))

        def quantize_b(j, parts=1):
            src = staged["b", j].bitcast(BF16)
            width = SIDES * PASSES * P // parts
            for part in range(parts):
                cols = slice(part * width, (part + 1) * width)
                nc.vector.quantize_mx(
                    out=b_codes[j][:, cols].bitcast(FP8X4),
                    scales=b_scale_rows[j][:, cols],
                    in_=src[:, PACK * cols.start : PACK * cols.stop],
                )

        def widen_x(j, on_vector):
            g, t = divmod(j, PACK)
            src = x_raw[j // 2][:, (j % 2) * D : (j % 2 + 1) * D].bitcast(FP8)
            dst = x_wide[g][:, t * D : (t + 1) * D]
            if on_vector:
                nc.vector.tensor_scalar(out=dst, in0=src, scalar1=x_scale_sb[:, j : j + 1], scalar2=None, op0=ALU.mult)
            else:
                nc.scalar.activation(out=dst, in_=src, func=ACT.Copy, scale=x_scale_sb[:, j : j + 1])

        def x_views(g, half, where, lo, hi):
            staged["x", g, half] = where
            src = x_wide[g][:].rearrange("p (t a d) -> p a t d", t=PACK, a=2)[:, half, :, lo:hi]
            return src, where.bitcast(BF16)[:, PACK * lo : PACK * hi]

        def weave_x(copy, g, half, where, lo=0, hi=D // 2):
            src, dst = x_views(g, half, where, lo, hi)
            copy(out=dst.rearrange("p (c i t) -> p c t i", t=PACK, i=RUN), in_=src.rearrange("p t (c i) -> p c t i", i=RUN))

        def weave_x_gpsimd(g, half, where, lo, hi):
            src, dst = x_views(g, half, where, lo, hi)
            nc.gpsimd.tensor_scalar(
                out=dst.rearrange("p (d t) -> p d t", t=PACK),
                in0=src.rearrange("p t d -> p d t"),
                scalar1=1.0,
                scalar2=0.0,
                op0=ALU.mult,
                op1=ALU.add,
            )

        def quantize_x(g, half):
            cols = slice(half * D // 2, (half + 1) * D // 2)
            nc.vector.quantize_mx(
                out=x_codes[g][:, cols].bitcast(FP8X4), scales=x_scale_rows[g][:, cols], in_=staged["x", g, half].bitcast(BF16)
            )

        def drives(j, c, number):
            bank = bank_tile(number, [P, SIDES, CHUNK])
            half, c0 = divmod(c * CHUNK, H // 2)
            for side in range(SIDES):
                for g in range(PASSES):
                    cols = slice((side * PASSES + g) * P, (side * PASSES + g + 1) * P)
                    nc.tensor.matmul_mx(
                        out=bank[:, side, :],
                        lhsT=b_codes[j][:, cols].bitcast(FP8X4),
                        lhsT_scale=b_scale_rows[j][:, cols],
                        rhs=y_codes[half][:, g, c0 : c0 + CHUNK].bitcast(FP8X4),
                        rhs_scale=y_scale_rows[:, g, c * CHUNK : (c + 1) * CHUNK],
                        start=(g == 0),
                        stop=(g == PASSES - 1),
                    )
            banks["drive", j, c] = bank

        def gate(pre, slot, j, h0, width):
            c, c0 = divmod(h0, CHUNK)
            nc.vector.scalar_tensor_tensor(
                out=pre[:, :, slot * width : (slot + 1) * width],
                in0=e_rows[j][:, h0 : h0 + width].unsqueeze(1).broadcast_to([P, SIDES, width]),
                scalar=1.0,
                in1=banks["drive", j, c][:, :, c0 : c0 + width],
                op0=ALU.subtract,
                op1=ALU.mult,
            )

        def step_tiles(width):
            pre = stream.tile([P, SIDES, width], F32, name="pre")
            prob = stream.tile([P, SIDES, width], F32, name="prob")
            return pre, prob

        def sigmoid(prob, pre, lo, hi):
            nc.scalar.activation(out=prob[:, :, lo:hi], in_=pre[:, :, lo:hi], func=ACT.Sigmoid, scale=-4.0)

        def difference(engine, dp, prob, lo, hi):
            engine.tensor_tensor(out=dp[:, lo:hi], in0=prob[:, 0, lo:hi], in1=prob[:, 1, lo:hi], op=ALU.subtract)

        def modulation(g, s, number):
            bank = bank_tile(number, [P, PACK, STRIP])
            for t in range(PACK):
                j = g * PACK + t
                nc.tensor.matmul(bank[:, t, :], lhsT=m_diag[:, j, :], rhs=e_rows[j][:, s * STRIP : (s + 1) * STRIP], start=True, stop=True)
            banks["mod", g, s] = bank

        def delta(g, s, dp, woven):
            nc.vector.tensor_tensor(
                out=woven.rearrange("p (c i t) -> p c t i", t=PACK, i=RUN),
                in0=dp.rearrange("p t (c i) -> p c t i", i=RUN),
                in1=banks["mod", g, s][:].rearrange("p t (c i) -> p c t i", i=RUN),
                op=ALU.mult,
            )

        def quantize_delta(g, h0, width, woven):
            cols = slice(h0, h0 + width)
            nc.vector.quantize_mx(out=delta_codes[g][:, cols].bitcast(FP8X4), scales=delta_scale_rows[g][:, cols], in_=woven)

        def update(h0, width, i0, count, number):
            bank = bank_tile(number, [P, count, width])
            for i in range(count):
                rows = slice((i0 + i) * P, (i0 + i + 1) * P)
                for g in range(PASSES):
                    nc.tensor.matmul_mx(
                        out=bank[:, i, :],
                        lhsT=x_codes[g][:, rows].bitcast(FP8X4),
                        lhsT_scale=x_scale_rows[g][:, rows],
                        rhs=delta_codes[g][:, h0 : h0 + width].bitcast(FP8X4),
                        rhs_scale=delta_scale_rows[g][:, h0 : h0 + width],
                        start=(g == 0),
                        stop=(g == PASSES - 1),
                    )
            banks["update", h0, i0] = bank

        def finish(h0, width, i0, count, on_vector=False):
            result = stream.tile([P, count, width], F32, name="result", bufs=10)
            bank = banks["update", h0, i0]
            if on_vector:
                nc.vector.tensor_scalar(out=result[:], in0=bank[:], scalar1=OUT_SCALE, scalar2=None, op0=ALU.mult)
            else:
                nc.scalar.activation(out=result[:], in_=bank[:], func=ACT.Copy, scale=OUT_SCALE)
            rows = out.rearrange("(i p) h -> p i h", p=P)[:, i0 : i0 + count, h0 : h0 + width]
            nc.sync.dma_start(out=rows, in_=result[:])

        def update_pair(c, first, numbers):
            for n, number in enumerate(numbers):
                update(c * CHUNK, CHUNK, first + 2 * n, 2, number)

        def finish_pair(c, first):
            for n in range(2):
                finish(c * CHUNK, CHUNK, first + 2 * n, 2)

        nc.gpsimd.dma_start(out=m_sb[:].rearrange("p (g t) -> p g t", t=PACK), in_=m.rearrange("(g p t) -> p g t", p=P, t=PACK))
        nc.gpsimd.dma_start(
            out=x_scale_sb[:].rearrange("p (g t) -> p g t", t=PACK), in_=x_scale.rearrange("(g p t) o -> p g (t o)", p=P, t=PACK)
        )
        make_identity(nc, identity[:])
        nc.vector.memset(zeros[:], 0.0)
        nc.vector.memset(y_scale_rows[:].rearrange("p g n -> p (g n)").bitcast(I32), 0)
        load_b(0)
        load_x(0)
        load_y(0)
        for quadrant in range(4):
            nc.scalar.dma_start(
                out=y_scale_rows[32 * quadrant : 32 * quadrant + 4].bitcast(I32),
                in_=y_scales[:, 4 * quadrant : 4 * quadrant + 4, :].rearrange("g r n -> r g n").bitcast(I32),
            )
        nc.scalar.activation(out=table_probe[:], in_=zeros[:, :2], func=ACT.Sigmoid)
        load_x(1)
        load_e(0)
        load_b(1)
        load_y(1)
        for t in range(1, PACK):
            load_b(2 * t)
            load_e(t)
            load_b(2 * t + 1)
            if t < PACK - 1:
                load_x(t + 1)
        nc.sync.dma_start(out=e_second[:], in_=e.rearrange("(g p t) h -> g p (t h)", p=P, t=PACK)[1])

        nc.vector.tensor_tensor(
            out=m_diag[:],
            in0=identity[:].unsqueeze(1).broadcast_to([P, TILES, P]),
            in1=m_sb[:].unsqueeze(2).broadcast_to([P, TILES, P]),
            op=ALU.mult,
        )
        warm_up(3)
        turn(0)
        warm_up(3)
        empty_turn(0, stage_tile())
        widen_x(0, on_vector=True)
        quantize_b(0, parts=SIDES)
        widen_x(1, on_vector=False)
        widen_x(2, on_vector=True)
        widen_x(3, on_vector=False)
        drives(0, 0, DRIVE_BANKS[0])
        drives(0, 1, DRIVE_BANKS[1])
        turn(1)
        warm_up(1)
        empty_turn(1, stage_tile())
        drives(0, 2, DRIVE_BANKS[2])
        drives(0, 3, DRIVE_BANKS[3])

        dp_part = [dp_first[:, t * H : (t + 1) * H] for t in range(PACK)]

        pre, prob = step_tiles(H)
        gate(pre, 0, 0, 0, CHUNK)
        gate(pre, 1, 0, CHUNK, CHUNK)
        weave_x(nc.vector.tensor_copy, 0, 0, dp_part[0])
        quantize_b(1)
        turn(2)
        drives(1, 0, DRIVE_BANKS[0])
        drives(1, 1, DRIVE_BANKS[1])
        sigmoid(prob, pre, 0, H // 2)
        empty_turn(2, stage_tile())
        for c in range(2, CHUNKS):
            gate(pre, c, 0, c * CHUNK, CHUNK)
            if c == CHUNKS - 1:
                sigmoid(prob, pre, H // 2, H)
            drives(1, c, DRIVE_BANKS[c])
        weave_x(nc.vector.tensor_copy, 0, 1, stage_tile())
        quantize_x(0, 0)
        quantize_b(2)
        widen_x(4, on_vector=False)
        difference(nc.gpsimd, dp_part[0], prob, 0, H)

        def first_pass_gates(t, where):
            pre, prob = step_tiles(H)
            turn(2 * t + 1)
            empty_turn(2 * t + 1, where)
            for c in range(CHUNKS):
                gate(pre, c, t, c * CHUNK, CHUNK)
                if c % 2 == 1:
                    sigmoid(prob, pre, (c - 1) * CHUNK, (c + 1) * CHUNK)
                if t == PACK - 1:
                    if c < 2:
                        drives(PACK + c, 0, DRIVE_BANKS[c])
                elif c == 1:
                    drives(t + 1, 0, DRIVE_BANKS[0])
                    drives(t + 1, 1, DRIVE_BANKS[1])
                    turn(2 * t + 2)
                elif c > 1:
                    drives(t + 1, c, DRIVE_BANKS[c])
            if t < PACK - 1:
                empty_turn(2 * t + 2, dp_part[t + 1])
            return prob

        prob = first_pass_gates(1, dp_part[1])
        widen_x(5, on_vector=True)
        quantize_b(3)
        quantize_x(0, 1)
        difference(nc.gpsimd, dp_part[1], prob, 0, H)

        prob = first_pass_gates(2, stage_tile())
        widen_x(6, on_vector=True)
        widen_x(7, on_vector=True)
        quantize_b(4)
        quantize_b(5)
        difference(nc.gpsimd, dp_part[2], prob, 0, H)

        prob = first_pass_gates(3, stage_tile())
        for t in range(2, PACK):
            quantize_b(PACK + t)
            drives(PACK + t, 0, DRIVE_BANKS[t])
        difference(nc.gpsimd, dp_part[3], prob, 0, CHUNK)
        difference(nc.gpsimd, dp_part[3], prob, CHUNK, H)

        dp_tiles = dp_first[:].rearrange("p (t h) -> p t h", t=PACK)
        work = [kept("work%d" % c, [P, H], F32) for c in range(CHUNKS + 1)]

        def woven_first(c):
            return work[c][:].bitcast(BF16)[:, PACK * CHUNK :]

        def woven_second(c):
            return work[c + 2][:].bitcast(BF16)[:, : PACK * CHUNK]

        def delta_first(s):
            c, a = divmod(s, 2)
            delta(0, s, dp_tiles[:, :, s * STRIP : (s + 1) * STRIP], woven_first(c)[:, a * BANK : (a + 1) * BANK])

        def delta_second(s):
            c, a = divmod(s, 2)
            dp = work[c][:].rearrange("p (t h) -> p t h", t=PACK)[:, :, a * STRIP : (a + 1) * STRIP]
            delta(1, s, dp, woven_second(c)[:, a * BANK : (a + 1) * BANK])

        def gate_second(pre, t, c):
            gate(pre, t, PACK + t, c * CHUNK, CHUNK)

        def drives_second(t, c):
            drives(PACK + t, c, DRIVE_BANKS[t])

        quarter = D // 4
        modulation(0, 0, MOD_BANKS[0])
        modulation(0, 1, MOD_BANKS[1])
        pre, prob = step_tiles(H)
        woven_x = [stage_tile(), stage_tile()]
        weave_x(nc.scalar.copy, 1, 0, woven_x[0], 0, quarter)
        for t in range(PACK):
            gate_second(pre, t, 0)
            if t % 2 == 1:
                sigmoid(prob, pre, (t - 1) * CHUNK, (t + 1) * CHUNK)
            if t < PACK - 1:
                drives_second(t, 1)
        delta_first(0)
        modulation(0, 2, MOD_BANKS[0])
        drives_second(PACK - 1, 1)
        delta_first(1)
        modulation(0, 3, MOD_BANKS[1])

        def second_pass_rest(c, pre, prob, next_mods, updating):
            drives_second(0, c + 1)
            delta_first(2 * c)
            modulation(1, 2 * c - 2, MOD_BANKS[0])
            gate_second(pre, 1, c)
            sigmoid(prob, pre, 0, H // 2)
            drives_second(1, c + 1)
            delta_first(2 * c + 1)
            modulation(1, 2 * c - 1, MOD_BANKS[1])
            if updating:
                update_pair(c - 2, PACK, OUT_BANKS)
            gate_second(pre, 2, c)
            drives_second(2, c + 1)
            gate_second(pre, 3, c)
            sigmoid(prob, pre, H // 2, H)
            if updating:
                finish_pair(c - 2, PACK)
            delta_second(2 * c - 2)
            modulation(*next_mods[0], MOD_BANKS[0])
            drives_second(3, c + 1)
            delta_second(2 * c - 1)
            modulation(*next_mods[1], MOD_BANKS[1])

        def second_pass_end(c, prob):
            quantize_delta(0, c * CHUNK, CHUNK, woven_first(c))
            quantize_delta(1, (c - 1) * CHUNK, CHUNK, woven_second(c - 1))
            difference(nc.gpsimd, work[c], prob, 0, H)

        prob_before = prob
        pre, prob = step_tiles(H)
        weave_x(nc.scalar.copy, 1, 0, woven_x[0], quarter, 2 * quarter)
        weave_x(nc.scalar.copy, 1, 1, woven_x[1], 0, quarter)
        gate_second(pre, 0, 1)
        quantize_delta(0, 0, CHUNK, woven_first(0))
        difference(nc.gpsimd, work[0], prob_before, 0, H)
        weave_x_gpsimd(1, 1, woven_x[1], quarter, 2 * quarter)
        second_pass_rest(1, pre, prob, [(0, 4), (0, 5)], updating=False)
        quantize_x(1, 0)
        quantize_x(1, 1)
        second_pass_end(1, prob)

        pre, prob = step_tiles(H)
        update_pair(0, 0, OUT_BANKS)
        finish_pair(0, 0)
        gate_second(pre, 0, 2)
        second_pass_rest(2, pre, prob, [(0, 6), (1, 4)], updating=True)
        second_pass_end(2, prob)

        near, last = 2 * CHUNKS - 2, 2 * CHUNKS - 1
        pre_near, prob_near = step_tiles(BANK)
        pre_last, prob_last = step_tiles(BANK)
        dp_strips = kept("dp_strips", [P, 2, BANK], F32)
        woven_strips = work[CHUNKS][:].bitcast(BF16)[:, PACK * CHUNK :].rearrange("p (a w) -> p a w", a=2)

        def gate_strip(pre, t, s):
            gate(pre, t, PACK + t, s * STRIP, STRIP)

        def delta_strip(s):
            a = s - near
            delta(1, s, dp_strips[:, a, :].rearrange("p (t h) -> p t h", t=PACK), woven_strips[:, a, :])

        update_pair(1, 0, OUT_BANKS)
        for t in range(PACK):
            gate_strip(pre_near, t, near)
            if t % 2 == 1:
                sigmoid(prob_near, pre_near, (t - 1) * STRIP, (t + 1) * STRIP)
        difference(nc.gpsimd, dp_strips[:, 0, :], prob_near, 0, BANK)
        finish_pair(1, 0)
        delta_first(near)
        modulation(1, near - 1, MOD_BANKS[0])
        gate_strip(pre_last, 0, last)
        gate_strip(pre_last, 1, last)
        sigmoid(prob_last, pre_last, 0, BANK // 2)
        update_pair(1, PACK, DRIVE_BANKS[:2])
        finish_pair(1, PACK)
        delta_second(near - 2)
        modulation(1, near, MOD_BANKS[1])
        delta_second(near - 1)
        modulation(0, last, MOD_BANKS[0])
        gate_strip(pre_last, 2, last)
        quantize_delta(1, 2 * CHUNK, CHUNK, woven_second(2))
        gate_strip(pre_last, 3, last)
        sigmoid(prob_last, pre_last, BANK // 2, BANK)
        update_pair(2, 0, OUT_BANKS)
        delta_strip(near)
        modulation(1, last, MOD_BANKS[1])
        update_pair(2, PACK, DRIVE_BANKS[2:])
        finish_pair(2, 0)
        finish_pair(2, PACK)
        delta_first(last)
        quantize_delta(1, near * STRIP, STRIP, woven_strips[:, 0, :])
        quantize_delta(0, 3 * CHUNK, CHUNK, woven_first(3))
        for n in range(2):
            update(near * STRIP, STRIP, PACK * n, PACK, DRIVE_BANKS[n])
        difference(nc.vector, dp_strips[:, 1, :], prob_last, 0, BANK)
        delta_strip(last)
        quantize_delta(1, last * STRIP, STRIP, woven_strips[:, 1, :])
        for n, number in enumerate((MOD_BANKS[0], OUT_BANKS[0], OUT_BANKS[1], DRIVE_BANKS[2])):
            update(last * STRIP, STRIP, 2 * n, 2, number)
        for n in range(2):
            finish(near * STRIP, STRIP, PACK * n, PACK, on_vector=(n == 1))
        for n in range(4):
            finish(last * STRIP, STRIP, 2 * n, 2, on_vector=(n % 2 == 1))
